import numpy as np, ml_dtypes
CORES = [24,25,26,27,28,29,30,31]
N = 8
BF = ml_dtypes.bfloat16
W, M, C, R, P = 3072, 2560, 256, 2, 2
def accounts(rng):
    H = W // 2; k = np.stack([rng.permutation(H) for _ in range(8)]); pw = rng.choice(np.array([1.0, 1.5, 2.0]), 8)
    c = np.minimum((H * rng.random((N, 8, 16 * M)) ** pw[None, :, None]).astype(np.int64), H - 1)
    e = (2 * k[np.arange(8)[None, :, None], c] + rng.integers(0, 2, c.shape)).reshape(N, 8, 16, M)
    none = (rng.random((N, 8, 16, M)) < 0.6 * rng.random((N, 8, 1, M)) ** 2) | (rng.random((N, 8, 1, M)) < 0.01)
    return np.where(none, W, e)
def keeps(rng):
    return rng.choice(np.array([0.0, 0.1, 0.3, 0.8]), (N, 8, 1, W // 2))
def books(rng, acct, keep):
    H = W // 2; out = rng.integers(0, M, (N, 8, 16, H)); m = np.tile(np.arange(M), 16)
    for q in range(N):
        for g in range(8):
            o = rng.permutation(16 * M); c = acct[q, g].reshape(-1)[o] >> 1
            s = np.argsort(c, kind="stable"); c = c[s]; who = m[o[s]]
            pos = np.arange(16 * M) - np.searchsorted(c, c)
            ok = (pos < 16) & (c < H) & (rng.random(16 * M) < keep[q, g, 0][np.minimum(c, H - 1)])
            out[q, g, pos[ok], c[ok]] = who[ok]
    return np.take_along_axis(out, np.argsort(rng.random(out.shape), axis=2), 2)
def losses(rng):
    return np.clip(np.rint(90 * rng.standard_normal((N, 8, 16, W), dtype=np.float32)), -255, 255).astype(np.int64)
def tops(loss, acct):
    x = np.take_along_axis(np.concatenate([loss, np.zeros((N, 8, 16, 1), np.int64)], axis=3), acct[..., :R * C].reshape(N, 8, 1, -1), 3)
    return np.max(np.add.reduce(x.reshape(N, 8, 16, 16, R * C), axis=3), axis=2)
def pack(loss, acct, book, cap):
    return {"loss": np.ascontiguousarray(loss.reshape(N, 128, W)).astype(np.float32).astype(BF), "acct": np.ascontiguousarray(acct.reshape(N, 128, M)).astype(np.int32),
            "book": np.ascontiguousarray(book.reshape(N, 128, W // 2)).astype(np.int32), "cap": np.ascontiguousarray(cap).astype(np.int32)}
def setup_inputs(rng):
    acct = accounts(rng)
    return pack(losses(rng), acct, books(rng, acct, keeps(rng)), rng.integers(0, 900, (N, 8, R * C)))
def setup_inputs_ties(rng):
    acct = accounts(rng); acct[:, ::2, 8:12] = acct[:, ::2, 0:4]
    loss = rng.integers(-2, 3, (N, 8, 16, W)) * rng.choice(np.array([1, 3, 100]), (N, 8, 1, 1)); loss[:, 1::2, 8:] = loss[:, 1::2, :8]
    loss[:, 6] = rng.integers(180, 255, (N, 1, 1)) + rng.integers(-1, 2, (N, 16, W))
    cap = np.clip(tops(loss, acct) + rng.choice(np.array([-1, -1, 0, 1]), (N, 8, R * C)), 0, 4095)
    keep = keeps(rng); keep[:, 6] = 0.8
    return pack(loss, acct, books(rng, acct, keep), cap)
def setup_inputs_crowd(rng):
    H = W // 2; acct = accounts(rng); loss = losses(rng); cap = rng.integers(0, 900, (N, 8, R * C))
    acct[:, 2:4] = 2 * rng.permutation(H)[:64][rng.integers(0, 64, (N, 2, 16, M))] + rng.integers(0, 2, (N, 2, 16, M))
    loss[:, :2] = rng.integers(-15, 16, (N, 2, 16, W)); cap[:, :2] = 0
    x = [int(2 * rng.integers(0, H)), int(2 * rng.integers(0, H) + 1)]; y = np.zeros((N, 2, 16), np.int64)
    for g in range(2):
        loss[:, g, :, x[g]] = 255
        for q in range(N):
            y[q, g] = R * C + rng.permutation(M - R * C)[:16]
            acct[q, g, rng.integers(0, 16, R * C), np.arange(R * C)] = x[g]
            acct[q, g, rng.integers(0, 16, 16), y[q, g]] = x[g] ^ 1
            acct[q, g, :, y[q, g, 1]] = x[g] ^ 1
    k = rng.permutation(H); e = 2 * k[:R * C] + rng.integers(0, 2, R * C); v = np.zeros((N, R * C), np.int64)
    acct[:, 4] = np.where(acct[:, 4] == W, W, 2 * k[rng.integers(R * C, H, (N, 16, M))] + rng.integers(0, 2, (N, 16, M)))
    big = rng.integers(-15, 16, (N, 16, W)); big[:, :, e] = rng.integers(240, 256, (N, 16, R * C)); loss[:, 4] = big; cap[:, 4] = 0
    for q in range(N):
        v[q] = R * C + rng.permutation(M - R * C)[:R * C]
        acct[q, 4, rng.integers(0, 16, R * C), np.arange(R * C)] = e
        acct[q, 4, rng.integers(0, 16, R * C), v[q]] = e ^ 1
    book = books(rng, acct, keeps(rng))
    for g in range(2):
        for q in range(N):
            book[q, g, :, x[g] >> 1] = y[q, g]; book[q, g, 0, x[g] >> 1] = rng.integers(0, R * C)
    for q in range(N): book[q, 4, rng.integers(0, 16, R * C), e >> 1] = v[q]
    return pack(loss, acct, book, cap)
def setup_inputs_ends(rng):
    H = W // 2; acct = accounts(rng); loss = losses(rng); cap = rng.integers(0, 300, (N, 8, R * C))
    acct[:, 0] = rng.choice(np.array([0, 1, W - 2, W - 1, W]), (N, 16, M))
    acct[:, 1, :, ::2] = acct[:, 1, :1, ::2]
    acct[:, 2:4, :, M - 1] = W
    acct[:, 4] = 2 * (rng.integers(-16, 16, (N, 16, M)) % H) + rng.integers(0, 2, (N, 16, M))
    acct[:, 5, 1:] = W
    acct[:, 6] = np.where(acct[:, 6] == W, rng.integers(0, W, (N, 16, M)), acct[:, 6]); loss[:, 6, 15] = 255
    cap[:, 6] = rng.choice(np.array([0, 4079, 4080, 4095]), (N, R * C))
    loss[:, 7, 1:] = -255
    book = books(rng, acct, np.full((N, 8, 1, H), 0.8))
    book[:, 2:4, :15] = M - 1
    book[:, 4] = rng.choice(np.array([0, M - 1, C - 1, C]), (N, 16, H))
    return pack(loss, acct, book, cap)
def setup_inputs_quiet(rng):
    acct = accounts(rng); cap = rng.integers(0, 900, (N, 8, R * C)); keep = keeps(rng); q = rng.permutation(N); g = rng.permutation(8)
    cap[q[0]] = 4095; cap[q[0], g[0]] = rng.integers(0, 300, R * C); cap[q[1]] = 0; cap[:, g[1]] = 4095
    keep[q[2]] = 0.0; keep[q[3]] = 1.0
    return pack(losses(rng), acct, books(rng, acct, keep), cap)
def setup_inputs_spread(rng):
    acct = rng.integers(0, W + 1, (N, 8, 16, M))
    loss = np.clip(np.rint(rng.standard_normal((N, 8, 16, W)) * np.exp2(rng.integers(0, 9, (N, 8, 1, W))) * (rng.random((N, 8, 1, W)) > 0.0625)), -255, 255).astype(np.int64)
    cap = np.exp2(12 * rng.random((N, 8, R * C))).astype(np.int64) - 1
    return pack(loss, acct, books(rng, acct, rng.random((N, 8, 1, W // 2))), cap)
def check_inputs(d):
    bad = []; v = np.asarray(d["loss"]).astype(np.float32)
    if not np.all((v >= -255) & (v <= 255) & (v == np.rint(v))): bad.append("whole numbers of loss")
    for k, hi in (("acct", W), ("book", M - 1), ("cap", 4095)):
        if np.min(d[k]) < 0 or np.max(d[k]) > hi: bad.append("range of " + k)
    return bad
def reference(loss, acct, book, cap):
    L = loss.astype(np.float32).astype(np.int64).reshape(N, 8, 16, W)
    L = np.concatenate([L, np.zeros((N, 8, 16, 1), np.int64)], axis=3)
    A = acct.astype(np.int64).reshape(N, 8, 16, M); B = book.astype(np.int64).reshape(N, 8, 16, W // 2); K = cap.astype(np.int64)
    said = np.zeros((N, 8, R * C), np.float32); slot = np.arange(C); rank = np.arange(N)[:, None]
    for t in range(R):
        lo = C * t
        mine = np.ascontiguousarray(A[..., lo:lo + C])
        x = np.take_along_axis(L, mine.reshape(N, 8, 1, 16 * C), 3).reshape(N, 8, 16, 16, C)
        z = np.add.reduce(x, axis=3)
        w = np.argmax(z, axis=2)
        over = np.max(z, axis=2) > K[..., lo:lo + C]
        xw = np.take_along_axis(x, w[:, :, None, None, :], 2)[:, :, 0]
        i = np.argmax(xw, axis=2)
        e = np.take_along_axis(mine, i[:, :, None], 2)[:, :, 0]
        d = 1 + (P * t + slot // (C // P)) % (N - 1)
        src = (rank - d) % N
        ok = over[src, :, slot].transpose(0, 2, 1)
        eo = np.where(ok, e[src, :, slot].transpose(0, 2, 1), 0); opp = eo ^ 1
        cand = np.take_along_axis(B, (eo >> 1)[:, :, None], 3)
        held = np.take_along_axis(A, cand.reshape(N, 8, 1, 16 * C), 3).reshape(N, 8, 16, 16, C)
        holds = np.any(held == opp[:, :, None, None], axis=2)
        found = ok & np.any(holds, axis=2)
        h = np.take_along_axis(cand, np.argmax(holds, axis=2)[:, :, None], 2)[:, :, 0]
        h = np.where(found, h, M + slot)
        same = (h[..., :, None] == h[..., None, :]) & (slot[None, :] < slot[:, None])
        acc = found & ~np.any(same, axis=-1)
        col = np.take_along_axis(A, np.where(acc, h, 0)[:, :, None], 3); new = np.where(col == opp[:, :, None], W, col)
        A = np.concatenate([A, np.zeros((N, 8, 16, C), np.int64)], axis=3)
        np.put_along_axis(A, np.ascontiguousarray(np.broadcast_to(np.where(acc, h, M + slot)[:, :, None], new.shape)), new, 3)
        A = np.ascontiguousarray(A[..., :M])
        back = acc[(rank + d) % N, :, slot].transpose(0, 2, 1)
        hit = back[:, :, None] & (np.arange(16)[None, None, :, None] == i[:, :, None])
        A[..., lo:lo + C] = np.where(hit, W, A[..., lo:lo + C])
        said[..., lo:lo + C] = over.astype(np.int64) + back.astype(np.int64)
    return {"left": (A < W).reshape(N, 128, M).astype(np.float32).astype(BF), "said": said}

@@ -1,0 +1,445 @@
+from concourse.bass import DstId, RemoteDMATransfer
+from concourse.mybir import AluOpType, ActivationFunctionType
+
+F, B, I, U, H = "float32", "bfloat16", "int32", "uint16", "float16"
+N = 8
+CH = 258
+NONE = 3072
+FLOOR = 15 * 4096 + NONE
+
+_SB = {
+    B: "L:3088 ONE:160 Sh:160 W0b:160 W1b:160 B15:128 BO:128 BO5:128 LO:128 LD:128 I4:128 I3:128 In:128 Ih:128 E:144 "
+       "DG:272 DX:256 PAY:256 RM:256 OV:272 th0:256 th1:256 THR:256 X0:4096 X1:4096 XT0:4128 XT1:4128 OH0:256 OH1:256 "
+       "OV0:256 OV1:256 EQ:4112 NF:256 EQ2:16,256 ac0:256 ac1:256 AC0:256 AC1:256 eqb:256 Pen:8,2,16 LF:2816 lc:256 LG:256",
+    F: "capF:32 capT:32 col:12 idf:128 W0f:160 W1f:160 BOf:128 C16:16 DM:16 pw:16 pm:16 OPP:3088 C0:256 C1:256 "
+       "Af0:8,2,16 Af1:8,2,16 AKs:256 K1:256 K2a:256 K2b:256 K2:256 t4:16 v4:16 cF:256 Eb:256 IN1:4096 K3a:256 K3:256 "
+       "OHc:256 hc:256 HD:256 V1:256 Fk:256 F2:16 eqf:256 cn:256 r32:2,2,8 q1:2,8 q2:2,8 Lo:256 Y:2816 YT:256 Zc:256 "
+       "sd0:256 sd1:256",
+    I: "A:2816 BK:1544 capI:32 PL:16 PLa:16 CL:32 BL:256 DGi:256 Ki:16 Kf:16 KI:2,8 M32:2,2,8 f4:16 nc:256",
+    U: "PLu:16 CLu:32 BLu:256 Off:512 o1:16 MU0:32 MU1:32 R0:32 R1:32 pio:16 cP:256 jo:16 EO:16 HO:16 SO:16 oo:16",
+    H: "h16:256",
+}
+SCRATCH = {e.split(":")[0]: ("sbuf", [128] + [int(x) for x in e.split(":")[1].split(",")], dt)
+           for dt, names in _SB.items() for e in names.split()}
+SCRATCH.update({k: ("psum", [128, 512], F) for k in ("Z0", "Z1", "CNT", "HR", "G", "CN")})
+SCRATCH.update({k: ("psum", [128, 16, 2, 16], F) for k in ("AK0", "AK1")})
+DMAS = ["dA0", "dL", "dcap", "dA2", "dBK", "o0", "o1", "o2", "o3", "o4"]
+SEMAPHORES = ["cV", "cS", "cP", "cG", "sent", "arr0", "arr1", "ack0", "ack1"] + DMAS
+
+
+def _emit(ops, queues, T):
+    writer, readers, bank = {}, {}, {}
+    known = {q: set() for q in queues}
+    snap, waits, needed = [], [], set()
+    earlier = {q: [] for q in queues}
+    for n, (q, fn, rd, wr, sem) in enumerate(ops):
+        deps = set()
+        for k in rd + wr:
+            if k in writer:
+                deps.add(writer[k])
+            if k[0] == "@":
+                deps.update(m for e, m in bank.get(k, {}).items() if e != q)
+        for k in wr:
+            deps.update(readers.get(k, []))
+        mine = []
+        for m in sorted(deps, reverse=True):
+            if m in known[q] or (q == "P" and ops[m][0] == "P"):
+                continue
+            mine.append(m)
+            needed.add(m)
+            known[q] |= snap[m]
+        waits.append(mine)
+        for k in rd:
+            readers.setdefault(k, []).append(n)
+        for k in wr:
+            writer[k] = n
+            readers[k] = []
+        for k in rd + wr:
+            if k[0] == "@":
+                bank.setdefault(k, {})[q] = n
+        if sem is None:
+            earlier[q].append(n)
+            snap.append(known[q] | set(earlier[q]))
+        else:
+            snap.append(known[q] | {n})
+    count, at = {q: 0 for q in queues}, {}
+    for n, (q, fn, rd, wr, sem) in enumerate(ops):
+        if sem is not None:
+            at[n] = (sem, 16)
+        elif n in needed:
+            count[q] += 1
+            at[n] = ("c" + q, count[q])
+    for n, (q, fn, rd, wr, sem) in enumerate(ops):
+        for m in waits[n]:
+            queues[q].wait_ge(T.sem[at[m][0]], at[m][1])
+        if fn is None:
+            continue
+        ins = fn()
+        if ins is None:
+            continue
+        if sem is not None:
+            ins.then_inc(T.sem[sem], 16)
+        elif n in needed:
+            ins.then_inc(T.sem["c" + q], 1)
+
+
+def rank_program(g, core, T, topo):
+    rank = T.rank_of(core)
+    if rank is None:
+        return
+    A_ = AluOpType
+    ID, RELU, SIGN = ActivationFunctionType.Identity, ActivationFunctionType.Relu, ActivationFunctionType.Sign
+    V, S, P = g.vector, g.scalar, g.tensor
+    ops = []
+
+    def add(q, fn, rd, wr, sem=None):
+        ops.append((q, fn, rd.split(), wr.split(), sem))
+
+    def memset(ap, c, wr):
+        add("V", lambda: V.memset(ap, c), "", wr)
+
+    def copy(o, i, rd, wr):
+        add("V", lambda: V.tensor_copy(o, i), rd, wr)
+
+    def ts(o, i, s1, o0, rd, wr, s2=None, o1=None):
+        if o1 is None:
+            add("V", lambda: V.tensor_scalar(o, i, s1, None, o0), rd, wr)
+        else:
+            add("V", lambda: V.tensor_scalar(o, i, s1, s2, o0, o1), rd, wr)
+
+    def tt(o, a, b, op, rd, wr):
+        add("V", lambda: V.tensor_tensor(o, a, b, op), rd, wr)
+
+    def scan(o, d0, d1, o0, o1, rd, wr):
+        add("V", lambda: V.tensor_tensor_scan(o, d0, d1, 0.0, o0, o1), rd, wr)
+
+    def segmax(o, i, rd, wr):
+        scan(o, T.RM[:], i, A_.mult, A_.max, rd + " RM", wr)
+
+    def turn(o, i, rd, wr):
+        add("V", lambda: V.transpose(o, i), rd, wr)
+
+    def act(o, i, rd, wr, scale=1.0, bias=0.0, func=ID):
+        add("S", lambda: S.activation(o, i, func, bias=bias, scale=scale), rd, wr)
+
+    def mm(o, l, r, start, stop, rd, wr):
+        add("P", lambda: P.matmul(o, l, r, start, stop), rd, wr)
+
+    def iota(o, pat, base, cm, wr, small=False):
+        if small:
+            add("G", lambda: g.iota(o, pat, base, cm, allow_small_or_imprecise_dtypes=True), "", wr)
+        else:
+            add("G", lambda: g.iota(o, pat, base, cm), "", wr)
+
+    def sel(o, i, pat, cmp, base, cm, rd, wr):
+        add("G", lambda: g.affine_select(o, i, pat, cmp, 0.0, base, cm), rd, wr)
+
+    def dma(q, o, i, rd, wr, sem):
+        add(q, lambda: (g.sync if q == "Y" else g.scalar).dma_start(o, i), rd, wr, sem)
+
+    def send(src, dst, width, peers, sem, rd):
+        trs = []
+        for b, peer in enumerate(peers):
+            c = T.cores[peer % N]
+            eng = topo.engines(core, c)
+            half = eng[b * len(eng) // 2:(b + 1) * len(eng) // 2]
+            rid, pid = topo.addr(c)[:2]
+            trs.append(RemoteDMATransfer(dst_ids=[DstId(rid=rid, pnc=pid)], dma_engine_mask=sum(1 << e for e in half),
+                                         remote_sem=T.sem[sem], src=src[:, b * width:(b + 1) * width],
+                                         dst=dst[:, b * width:(b + 1) * width]))
+
+        def go():
+            g.remote_dma_fused(trs, local_sem=T.sem.sent)
+        add("G", go, rd, "")
+
+    for t in range(2):
+        add("G", None, "", "R%d" % t, "arr%d" % t)
+        add("G", None, "", "AC%d" % t, "ack%d" % t)
+
+    dma("Y", T.A[:, 256:768], T.acct[:, 0:512], "", "A0 A1 go", "dA0")
+    dma("S", T.capI[:], T.cap[:, :], "", "capI", "dcap")
+    dma("Y", T.L[:, 0:3072], T.loss[:, :], "", "L", "dL")
+    dma("Y", T.BK[:, 0:1536], T.book[:, :], "go", "BK", "dBK")
+    dma("Y", T.A[:, 768:2816], T.acct[:, 512:2560], "", "A2", "dA2")
+
+    iota(T.PL[:], [[1, 16]], 0, 16, "PL")
+    iota(T.ONE[:], [[0, 160]], 1, 0, "ONE", True)
+    sel(T.Sh[:], T.ONE[:], [[-1, 160]], A_.is_equal, 16, 1, "ONE", "Sh")
+    iota(T.CL[:], [[8, 2], [1, 8], [16, 2]], 0, 0, "CL")
+    iota(T.DGi[:], [[-1, 256]], 256, 1, "DGi")
+    sel(T.BO[:], T.ONE[:, 0:128], [[-16, 8], [0, 16]], A_.is_ge, 0, 1, "ONE", "BO")
+    iota(T.PAY[:], [[-1, 256]], 256, 0, "PAY", True)
+    sel(T.BO[:], T.BO[:], [[16, 8], [0, 16]], A_.is_ge, 15, -1, "BO", "BO")
+    iota(T.BL[:], [[1, 16], [16, 16]], 0, 0, "BL")
+    iota(T.C16[:], [[16, 16]], 0, 0, "C16", True)
+    iota(T.OPP[:], [[2, 1544], [-1, 2]], 1, 0, "OPP", True)
+    idb = T.Sh[:, 16:144]
+    r16, m1, m0, colr, colE, b15, colD, n0, n1 = [T.col[:, k:k + 1] for k in range(9)]
+
+    memset(T.RM[:], 1.0, "RM")
+    memset(T.OV[:, 0:256], 1.0, "OV")
+    ts(T.PLa[:], T.PL[:], 255, A_.bitwise_and, "PL", "PLa")
+    ts(T.f4[:, 0:1], T.PL[:, 0:1], 8, A_.arith_shift_right, "PL", "f4", 1, A_.bitwise_and)
+    memset(T.th0[:], 0.5, "th0")
+    memset(T.th1[:], 0.0, "th1")
+    copy(m1, T.f4[:, 0:1], "f4", "m1")
+    copy(r16, T.PLa[:, 0:1], "PLa", "r16")
+    copy(T.PLu[:], T.PLa[:], "PLa", "PLu")
+    ts(m0, m1, -1.0, A_.mult, "m1", "m0", 1.0, A_.add)
+    ts(n1, m1, 2.0 ** -16, A_.mult, "m1", "n1")
+    ts(n0, m1, -2.0 ** -16, A_.mult, "m1", "n0", 2.0 ** -16, A_.add)
+    ts(b15, r16, -1.0 / 256, A_.mult, "r16", "b15", 15.0 / 16, A_.add)
+    memset(T.RM[:, 0::16], 0.0, "RM")
+    memset(T.th0[:, 0::16], 0.0, "th0")
+    memset(T.th1[:, 0::16], -2.0 ** 28, "th1")
+    memset(T.L[:, 3072:3088], 0.0, "Lp")
+    memset(T.OV[:, 256:272], 0.0, "OVp")
+    memset(T.E[:], 0.0, "E")
+    for x in (T.XT0, T.XT1):
+        memset(x[:, 256::CH], 0.0, x.name + "p")
+        memset(x[:, 257::CH], 0.0, x.name + "q")
+    scan(T.THR[:], T.th0[:], T.th1[:], A_.mult, A_.add, "th0 th1", "THR")
+    copy(T.CLu[:], T.CL[:], "CL", "CLu")
+    copy(T.capF[:], T.capI[:], "capI", "capF")
+    ts(colr, r16, CH / 16.0, A_.mult, "r16", "colr", 256.0, A_.add)
+    ts(colE, r16, 16.0, A_.mult, "r16", "colE", 256.0, A_.add)
+    turn(T.capT[:], T.capF[:], "capF", "capT")
+    ts(colD, r16, 1.0 / 16, A_.mult, "r16", "colD", 3841.0, A_.add)
+    memset(T.BK[:, 1536:1544], 0, "BKp")
+    memset(T.DG[:, 256:272], 0.0, "DGp")
+    memset(T.EQ[:, 4096:4112], 0.0, "EQp")
+    ts(T.DGi[:], T.DGi[:], 15, A_.bitwise_and, "DGi", "DGi")
+    copy(T.Off[:, 0:256], T.A[:, 256:512].indirect(T.PLu[:, 0:16]), "A0 PLu", "Off0")
+    copy(T.Af0[:], T.A[:, 256:512], "A0", "Af0")
+    ts(T.DG[:, 0:256], T.DGi[:], 0.0, A_.is_equal, "DGi", "DG")
+    ts(T.E[:, 15:143:16], T.BO[:, 0::16], 512.0, A_.mult, "BO", "E")
+    copy(T.Off[:, 256:512], T.A[:, 512:768].indirect(T.PLu[:, 0:16]), "A1 PLu", "Off1")
+    tt(T.pw[:], T.THR[:, 0:16], T.DG[:, 0:16], A_.mult, "THR DG", "pw")
+    copy(T.Af1[:], T.A[:, 512:768], "A1", "Af1")
+    scan(T.pm[:], T.pw[:], T.pw[:], A_.min, A_.min, "pw", "pm")
+    act(T.B15[:], idb, "Sh b15", "B15", b15)
+    act(T.W0f[:], T.Sh[:], "Sh n0", "W0f", n0)
+    act(T.W1f[:], T.Sh[:], "Sh n1", "W1f", n1)
+    act(T.idf[:], idb, "Sh", "idf")
+    act(T.I4[:], idb, "Sh", "I4", 4096.0)
+    act(T.In[:], idb, "Sh", "In", -2.0)
+
+    def capital(t):
+        act(T["C%d" % t][:], T.capT[:, 0:32].indirect(T.CLu[:, 16 * t:16 * t + 16]), "capT CLu", "C%d" % t, -512.0, -512.0)
+
+    def z_open(t):
+        z = T["Z%d" % t][:, 0:256]
+        mm(z, T.idf[:], T["C%d" % t][:], True, False, "idf C%d" % t, "@Z%d" % t)
+        mm(z, idb, T.PAY[:], False, False, "Sh PAY", "@Z%d" % t)
+
+    def swap(t, w0, w1, src, names, stop):
+        ak = T["AK%d" % t]
+        for u, be, l in ((0, 0, w0[:, 16:144]), (0, 1, w0[:, 0:128]), (1, 1, w1[:, 16:144]), (1, 0, w1[:, 32:160])):
+            mm(ak[:, 0:8, u, :], l, src[:, :, be, :], False, stop and u == 1 and be == 0, names, "@AK%d" % t)
+
+    def ak_open(t):
+        mm(T["AK%d" % t][:, 0:8, :, :], T.B15[:], T.OV[:, 0:256], True, False, "B15 OV", "@AK%d" % t)
+        swap(t, T.W0f, T.W1f, T["Af%d" % t], "W0f W1f Af%d" % t, t == 0)
+
+    def x_gather(q, t, r0, r1):
+        src = T.L[:, 0:3088].indirect(T.Off[:, 256 * t + 16 * r0:256 * t + 16 * r1])
+        dst = T["X%d" % t][:, 256 * r0:256 * r1]
+        (copy if q == "V" else act)(dst, src, "L Lp Off%d" % t, " ".join("X%d.%d" % (t, r) for r in range(r0, r1)))
+
+    def x_turn(t, r):
+        xt = T["XT%d" % t][:, CH * r:CH * r + 256]
+        turn(xt, T["X%d" % t][:, 256 * r:256 * r + 256], "X%d.%d" % (t, r), "XT%d.%d" % (t, r))
+        mm(T["Z%d" % t][:, 0:256], T.E[:, 15 - r:143 - r], xt, False, r == 15, "E XT%d.%d" % (t, r), "@Z%d" % t)
+
+    def ak_out(t):
+        act(T.AKs[:], T["AK%d" % t][:, 0:8, :, :], "@AK%d" % t, "AKs")
+
+    def offers(t, z, zname):
+        xt = " ".join("XT%d.%d" % (t, r) for r in range(16)) + " XT%dp XT%dq" % (t, t)
+        segmax(T.K1[:], z, zname, "K1")
+        copy(T.Ki[:], T.K1[:, 15::16], "K1", "Ki")
+        ts(T.Kf[:], T.Ki[:], 511, A_.bitwise_and, "Ki", "Kf")
+        ts(T.o1[:], T.Kf[:], -1.0, A_.mult, "Kf colr", "o1", colr, A_.add)
+        tt(T.K2a[:], T["XT%d" % t][:, 0:16 * CH].indirect(T.o1[:, 0:16]), T.AKs[:], A_.add, xt + " o1 AKs", "K2a")
+        turn(T.K2b[:], T.K2a[:], "K2a", "K2b")
+        segmax(T.K2[:], T.K2b[:], "K2b", "K2")
+        ts(T.KI[:], T.K2[:, 15::16], 65536.0, A_.mult, "K2", "KI", float(FLOOR), A_.max)
+        ts(T.M32[:, :, 0, :], T.KI[:], 4095, A_.bitwise_and, "KI", "Me")
+        ts(T.M32[:, :, 1, :], T.KI[:], 1, A_.arith_shift_right, "KI", "Mc", 2047, A_.bitwise_and)
+        copy(T["MU%d" % t][:], T.M32[:], "Me Mc", "MU%d" % t)
+        send(T["MU%d" % t], T["R%d" % t], 16, [rank + 1 + 2 * t, rank + 2 + 2 * t], "arr%d" % t, "MU%d" % t)
+
+    def offered():
+        ts(T.f4[:], T.KI[:], 12, A_.arith_shift_right, "KI", "f4", 15, A_.bitwise_and)
+        ts(T.t4[:], T.KI[:], 65536.0, A_.is_lt, "KI", "t4", 256.0, A_.mult)
+        tt(T.v4[:], T.t4[:], T.f4[:], A_.subtract, "t4 f4", "v4")
+        ts(T.pio[:], T.v4[:], 15.0, A_.add, "v4", "pio")
+
+    def offered_rows(t):
+        sc, bi = ((1.0, -1.0), (-2.0, 4.0))[t]
+        act(T["OH%d" % t][:], T.DG[:, 0:272].indirect(T.pio[:, 0:16]), "DG DGp pio", "OH%d" % t, sc, bi)
+        act(T["OV%d" % t][:], T.OV[:, 0:272].indirect(T.pio[:, 0:16]), "OV OVp pio", "OV%d" % t, 1.0, 0.5)
+
+    eq_all = " ".join("EQ.%d" % r for r in range(16)) + " EQp"
+    a_all = "Ad A0 A1 A2"
+    lf_all = "LFd LF0 LF1 LF2 LF3"
+
+    def holders(t):
+        R = T["R%d" % t]
+        rn = "R%d" % t
+        mm(T.HR[:, 0:256], T.I4[:], T.DG[:, 0:256], True, False, "I4 DG", "@HR")
+        mm(T.G[:, 0:256], T.In[:], T.THR[:], True, False, "In THR", "@G")
+        for b in range(2):
+            ts(T.cF[:, 128 * b:128 * b + 128], T.BK[:, 0:1544].indirect(R[:, 16 * b + 8:16 * b + 16]), 1.0, A_.add,
+               "BK BKp " + rn, "cF%d" % b)
+            act(T.Eb[:, 128 * b:128 * b + 128], T.OPP[:, 0:3088].indirect(R[:, 16 * b:16 * b + 8]), "OPP " + rn, "Eb%d" % b)
+        ts(T.cP[:], T.cF[:, 0:256].indirect(T.PLu[:, 0:16]), -1.0, A_.add, "cF0 cF1 PLu", "cP")
+        cuts = [0, 1, 2, 4, 6, 8, 10, 12, 14, 15, 16]
+        for r0, r1 in zip(cuts[:-1], cuts[1:]):
+            c0, c1 = 256 * r0, 256 * r1
+            act(T.IN1[:, c0:c1], T.Eb[:, 0:256].indirect(T.BLu[:, 16 * r0:16 * r1]), "Eb0 Eb1 BLu", "IN.%d" % r0)
+            tt(T.EQ[:, c0:c1], T.A[:, 256:2816].indirect(T.cP[:, 16 * r0:16 * r1]), T.IN1[:, c0:c1], A_.is_equal,
+               "A0 A1 A2 cP IN.%d" % r0, " ".join("EQ.%d" % r for r in range(r0, r1)))
+            for r in range(r0, r1):
+                mm(T.CNT[:, 0:256], T.E[:, 15 - r:143 - r], T.EQ[:, 256 * r:256 * r + 256], r == 0, r == 15,
+                   "E EQ.%d" % r, "@CNT")
+
+    def first_holder():
+        tt(T.K3a[:], T.CNT[:, 0:256], T.PAY[:], A_.min, "@CNT PAY", "K3a")
+        segmax(T.K3[:], T.K3a[:], "K3a", "K3")
+        ts(T.jo[:], T.K3[:, 15::16], -1.0, A_.mult, "K3", "jo", 256.0, A_.add)
+        ts(T.EO[:], T.K3[:, 15::16], -1.0, A_.mult, "K3 colE", "EO", colE, A_.add)
+        tt(T.OHc[:], T.DG[:, 0:272].indirect(T.jo[:, 0:16]), T.cF[:], A_.mult, "DG DGp jo cF0 cF1", "OHc")
+        mm(T.HR[:, 0:256], T.BOf[:], T.OHc[:], False, True, "BOf OHc", "@HR")
+
+    def compare():
+        tt(T.h16[:], T.HR[:, 0:256], T.DX[:], A_.subtract, "@HR DX", "h16")
+        segmax(T.hc[:], T.HR[:, 0:256], "@HR", "hc")
+        act(T.NF[:], T.HR[:, 0:256], "@HR", "NF", -1.0, 1.0, RELU)
+        act(T.HD[:], T.HR[:, 0:256], "@HR", "HD")
+        for c in range(16):
+            lo = 16 * c
+            ts(T.EQ2[:, c, 0:256 - lo], T.h16[:, lo:256], 5376.0, A_.add, "h16 hc", "E2.%d" % c,
+               T.hc[:, lo + 15:lo + 16], A_.is_equal)
+            if c == 0:
+                ts(T.HO[:], T.hc[:, 15::16], -3841.0, A_.add, "hc", "HO")
+            if c < 15:
+                mm(T.G[:, lo + 16:256], T.LO[:], T.EQ2[:, c, 16:256 - lo], False, False, "LO E2.%d" % c, "@G")
+            if c == 11:
+                mm(T.G[:, 0:256], T.LO[:], T.NF[:], False, False, "LO NF", "@G")
+        mm(T.G[:, 0:256], T.LD[:], T.EQ2[:, :, 0:16], False, True, "LD " + " ".join("E2.%d" % c for c in range(16)), "@G")
+
+    def verdicts(t):
+        ac = T["ac%d" % t]
+        tt(T.V1[:], T.G[:, 0:256], T.HD[:], A_.min, "@G HD", "V1")
+        act(ac[:], T.V1[:], "V1", "ac%d" % t, 1.0, 0.0, SIGN)
+        send(ac, T["AC%d" % t], 128, [rank - 1 - 2 * t, rank - 2 - 2 * t], "ack%d" % t, "ac%d" % t)
+        segmax(T.Fk[:], T.V1[:], "V1", "Fk")
+        tt(T.F2[:], T.Fk[:, 15::16], T.DM[:], A_.max, "Fk DM", "F2")
+        ts(T.SO[:], T.F2[:], -3841.0, A_.add, "F2", "SO")
+
+    def said(t, q):
+        sd, ps = T["sd%d" % t], T.AK0[:, 0:8, :, :]
+        mm(ps, idb, T["OV%d" % t][:], True, False, "Sh OV%d" % t, "@AK0")
+        mm(ps, T.Ih[:], T["AC%d" % t][:], False, True, "Ih AC%d" % t, "@AK0")
+        act(sd[:], ps, "@AK0", "sd%d" % t)
+        dma(q, T.said[:, 256 * t:256 * t + 256], sd[0::16, :], "sd%d" % t, "out%d" % t, "o%d" % t)
+
+    def left(lo, hi, rd, wr):
+        ts(T.LF[:, lo:hi], T.A[:, lo:hi], float(NONE), A_.is_lt, rd, wr)
+
+    capital(0)
+    capital(1)
+    ak_open(0)
+    z_open(0)
+    act(T.DX[:], T.DG[:, 0:256], "DG", "DX", 4096.0, 1280.0)
+    ak_out(0)
+    x_gather("V", 0, 0, 3)
+    x_gather("V", 0, 3, 6)
+    for r0, r1 in ((6, 8), (8, 10), (10, 12), (12, 14), (14, 15), (15, 16)):
+        x_gather("S", 0, r0, r1)
+    for r in range(16):
+        x_turn(0, r)
+    for r0 in range(0, 10, 2):
+        x_gather("S", 1, r0, r0 + 2)
+    copy(T.BLu[:], T.BL[:], "BL", "BLu")
+    offers(0, T.Z0[:, 0:256], "@Z0")
+    ak_open(1)
+    z_open(1)
+
+    offered()
+    memset(T.A[:, 0:256], 0, "Ad")
+    for r in range(10):
+        x_turn(1, r)
+
+    holders(0)
+    act(T.BOf[:], T.BO[:], "BO", "BOf")
+    for r0 in (10, 12, 14):
+        x_gather("S", 1, r0, r0 + 2)
+    act(T.LO[:], T.BO[:], "BO", "LO", -2.0 ** 29)
+    act(T.LD[:], T.BO[:], "BO pm", "LD", T.pm[:, 15:16])
+    copy(T.r32[:], T.R0[:], "R0", "r32")
+    ts(T.q1[:], T.r32[:, :, 1, :], 4.0, A_.mult, "r32", "q1", 1.0, A_.add)
+    tt(T.q2[:], T.q1[:], T.r32[:, :, 0, :], A_.subtract, "q1 r32", "q2")
+    first_holder()
+    copy(T.oo[:], T.q2[:], "q2", "oo")
+    for r in range(10, 14):
+        x_turn(1, r)
+    eq = T.EQ[:, 0:4112].indirect(T.EO[:, 0:16])
+    act(T.eqf[:], eq, eq_all + " EO", "eqf", float(NONE))
+    compare()
+    act(T.eqb[:], eq, eq_all + " EO", "eqb")
+    act(T.BO5[:], T.BO[:], "BO", "BO5", 512.0)
+    act(T.DM[:], T.C16[:], "C16 colD", "DM", 1.0, colD)
+    mm(T.CN[:, 0:256], T.BO5[:], T.eqb[:], True, True, "BO5 eqb", "@CN")
+    act(T.Lo[:], T.L[:, 0:3088].indirect(T.oo[:, 0:16]), "L Lp oo", "Lo")
+    act(T.Y[:, 512:768], T.OV[:, 0:256], "OV", "Y", 0.0)
+    act(T.cn[:], T.CN[:, 0:256], "@CN", "cn")
+    tt(T.nc[:], T.A[:, 0:2816].indirect(T.HO[:, 0:16]), T.eqf[:], A_.max, a_all + " HO eqf", "nc")
+    x_turn(1, 14)
+    verdicts(0)
+    act(T.W0b[:], T.Sh[:], "Sh m0", "W0b", m0)
+    act(T.W1b[:], T.Sh[:], "Sh m1", "W1b", m1)
+    act(T.I3[:], idb, "Sh", "I3", float(NONE))
+    act(T.Ih[:], idb, "Sh", "Ih", 0.5)
+    act(T.LF[:, 0:256], T.OV[:, 0:256], "OV", "LFd", 0.0)
+    x_turn(1, 15)
+    copy(T.A[:, 0:2816].indirect(T.SO[:, 0:16]), T.nc[:], "nc SO", a_all)
+    tt(T.Y[:, 0:2816].indirect(T.SO[:, 0:16]), T.Lo[:], T.cn[:], A_.mult, "SO Lo cn", "Y")
+    ts(T.Pen[:], T.A[:, 512:768], float(NONE), A_.is_equal, "A1", "Pen", -512.0, A_.mult)
+    offered_rows(0)
+    swap(1, T.W0b, T.W1b, T.Pen, "W0b W1b Pen", True)
+    ak_out(1)
+
+    turn(T.YT[:], T.Y[:, 512:768], "Y", "YT")
+    tt(T.Zc[:], T.Z1[:, 0:256], T.YT[:], A_.subtract, "@Z1 YT", "Zc")
+    mm(T.Z0[:, 0:256], T.I3[:], T.OH0[:], True, False, "I3 OH0", "@Z0")
+    mm(T.Z0[:, 0:256], T.I3[:], T.AC0[:], False, True, "I3 AC0", "@Z0")
+    said(0, "Y")
+    offers(1, T.Zc[:], "Zc")
+    tt(T.A[:, 256:512], T.A[:, 256:512], T.Z0[:, 0:256], A_.max, "A0 @Z0", "A0")
+    offered()
+    offered_rows(1)
+    left(512, 1792, "A1 A2", "LF1")
+
+    holders(1)
+    left(256, 512, "A0", "LF0")
+    first_holder()
+    left(1792, 2304, "A2", "LF2")
+    act(T.eqb[:], eq, eq_all + " EO", "eqb", -1.0, 1.0)
+    compare()
+    left(2304, 2816, "A2", "LF3")
+    mm(T.Z0[:, 0:256], idb, T.OH1[:], True, False, "Sh OH1", "@Z0")
+    verdicts(1)
+    act(T.lc[:], T.LF[:, 0:2816].indirect(T.HO[:, 0:16]), lf_all + " HO", "lc")
+    tt(T.LF[:, 0:2816].indirect(T.SO[:, 0:16]), T.lc[:], T.eqb[:], A_.mult, "SO lc eqb", lf_all)
+    dma("Y", T.left[:, 512:2560], T.LF[:, 768:2816], "LF1 LF2 LF3", "out2", "o2")
+    dma("S", T.left[:, 0:256], T.LF[:, 256:512], "LF0", "out3", "o3")
+    mm(T.Z0[:, 0:256], T.In[:], T.AC1[:], False, True, "In AC1", "@Z0")
+    tt(T.LG[:], T.LF[:, 512:768], T.Z0[:, 0:256], A_.min, "LF1 @Z0", "LG")
+    dma("Y", T.left[:, 256:512], T.LG[:], "LG", "out4", "o4")
+    said(1, "S")
+    add("Y", None, "out0 out1 out2 out3 out4", "")
+
+    _emit(ops, {"V": V, "S": S, "P": P, "G": g, "Y": g.sync}, T)
+    g.wait_ge(T.sem.sent, 64)

@@ -6,23 +6,25 @@ N = 8
 CH = 258
 NONE = 3072
 FLOOR = 15 * 4096 + NONE
+BIG = 2 ** 23
+OWN = (56, 72)
 
 _SB = {
-    B: "L:3088 ONE:160 Sh:160 W0b:160 W1b:160 B15:128 BO:128 BO5:128 LO:128 LD:128 I4:128 I3:128 In:128 Ih:128 E:144 "
-       "DG:272 DX:256 PAY:256 RM:256 OV:272 th0:256 th1:256 THR:256 X0:4096 X1:4096 XT0:4128 XT1:4128 OH0:256 OH1:256 "
-       "OV0:256 OV1:256 EQ:4112 NF:256 EQ2:16,256 ac0:256 ac1:256 AC0:256 AC1:256 eqb:256 Pen:8,2,16 LF:2816 lc:256 LG:256",
-    F: "capF:32 capT:32 col:12 idf:128 W0f:160 W1f:160 BOf:128 C16:16 DM:16 pw:16 pm:16 OPP:3088 C0:256 C1:256 "
-       "Af0:8,2,16 Af1:8,2,16 AKs:256 K1:256 K2a:256 K2b:256 K2:256 t4:16 v4:16 cF:256 Eb:256 IN1:4096 K3a:256 K3:256 "
-       "OHc:256 hc:256 HD:256 V1:256 Fk:256 F2:16 eqf:256 cn:256 r32:2,2,8 q1:2,8 q2:2,8 Lo:256 Y:2816 YT:256 Zc:256 "
-       "sd0:256 sd1:256",
-    I: "A:2816 BK:1544 capI:32 PL:16 PLa:16 CL:32 BL:256 DGi:256 Ki:16 Kf:16 KI:2,8 M32:2,2,8 f4:16 nc:256",
-    U: "PLu:16 CLu:32 BLu:256 Off:512 o1:16 MU0:32 MU1:32 R0:32 R1:32 pio:16 cP:256 jo:16 EO:16 HO:16 SO:16 oo:16",
-    H: "h16:256",
+    B: "L:3088 ONE:160 Sh:160 W0b:160 W1b:160 B15:128 BO:128 BO5:128 BOa:128 BOq:128 LO:128 LT:128 E:144 D16:16 DR:16 "
+       "DG:256 DGc:256 DX:256 NEG:256 PAY:256 RM:256 OV:256 TH:16,17 Tab:8,32 WJ:2048 X0:4096 X1:4096 XT0:4128 XT1:4128 "
+       "OH0:256 OH1:256 OV0:256 OV1:256 EQ:4096 NF:16,17 EQ2:16,272 ac0:16,17 ac1:16,17 AC0:16,17 AC1:16,17 eqb:256 "
+       "Pen:8,2,16 LF:2816 lc:256 LG:256",
+    F: "capF:32 capT:32 col:12 idf:128 W0f:160 W1f:160 K16:16 OPP:3088 C0:256 C1:256 Af:2816 Ap0:8,2,16 Ap1:8,2,16 "
+       "AKs:256 K1:256 K2a:256 K2b:256 K2:256 Eb:256 RAW:4096 t32:256 hc:256 HD:272 Fk:272 Acol:256 eqf:256 cn:256 "
+       "r32:4,8 q1:16 q2:16 Lo:256 Y:2816 YT:256 Zc:256 sd0:256 sd1:256",
+    I: "A:2560 BK:1544 capI:32 PL:16 PLa:16 CL:32 Ki:16 Kf:16 KI:16 M32:4,8 f4:16",
+    U: "PLu:16 CLu:32 rl:16 Off:512 o1:16 MU0:32 MU1:32 R0:32 R1:32 pio:16 cP:256 HO:16 SO:16 oo:16",
+    H: "h17:16,17 c16:256 t16:256 BOh:128",
 }
 SCRATCH = {e.split(":")[0]: ("sbuf", [128] + [int(x) for x in e.split(":")[1].split(",")], dt)
            for dt, names in _SB.items() for e in names.split()}
-SCRATCH.update({k: ("psum", [128, 512], F) for k in ("Z0", "Z1", "CNT", "HR", "G", "CN")})
-SCRATCH.update({k: ("psum", [128, 16, 2, 16], F) for k in ("AK0", "AK1")})
+SCRATCH.update({k: ("psum", [128, 512], F) for k in ("Z0", "Z1", "SC", "HR", "G", "EB")})
+SCRATCH.update({k: ("psum", [128, 16, 32], F) for k in ("AK0", "AK1")})
 DMAS = ["dA0", "dL", "dcap", "dA2", "dBK", "o0", "o1", "o2", "o3", "o4"]
 SEMAPHORES = ["cV", "cS", "cP", "cG", "sent", "arr0", "arr1", "ack0", "ack1"] + DMAS
 
@@ -125,11 +127,14 @@ def rank_program(g, core, T, topo):
     def mm(o, l, r, start, stop, rd, wr):
         add("P", lambda: P.matmul(o, l, r, start, stop), rd, wr)
 
-    def iota(o, pat, base, cm, wr, small=False):
+    def iota(o, pat, base, cm, wr, small=True):
         if small:
             add("G", lambda: g.iota(o, pat, base, cm, allow_small_or_imprecise_dtypes=True), "", wr)
         else:
             add("G", lambda: g.iota(o, pat, base, cm), "", wr)
+
+    def fill(o, n, c, wr):
+        iota(o, [[0, n]], c, 0, wr)
 
     def sel(o, i, pat, cmp, base, cm, rd, wr):
         add("G", lambda: g.affine_select(o, i, pat, cmp, 0.0, base, cm), rd, wr)
@@ -156,73 +161,70 @@ def rank_program(g, core, T, topo):
         add("G", None, "", "R%d" % t, "arr%d" % t)
         add("G", None, "", "AC%d" % t, "ack%d" % t)
 
-    dma("Y", T.A[:, 256:768], T.acct[:, 0:512], "", "A0 A1 go", "dA0")
+    dma("Y", T.A[:, 0:512], T.acct[:, 0:512], "", "A01 go", "dA0")
     dma("S", T.capI[:], T.cap[:, :], "", "capI", "dcap")
     dma("Y", T.L[:, 0:3072], T.loss[:, :], "", "L", "dL")
-    dma("Y", T.BK[:, 0:1536], T.book[:, :], "go", "BK", "dBK")
-    dma("Y", T.A[:, 768:2816], T.acct[:, 512:2560], "", "A2", "dA2")
+    dma("Y", T.A[:, 512:2560], T.acct[:, 512:2560], "go", "A2", "dA2")
+    dma("Y", T.BK[:, 0:1536], T.book[:, :], "", "BK", "dBK")
 
-    iota(T.PL[:], [[1, 16]], 0, 16, "PL")
-    iota(T.ONE[:], [[0, 160]], 1, 0, "ONE", True)
+    iota(T.PL[:], [[1, 16]], 0, 16, "PL", False)
+    iota(T.OPP[:, 0:96], [[2, 48], [-1, 2]], 1, 0, "OPP0")
+    iota(T.CL[:], [[8, 2], [1, 8], [16, 2]], 0, 0, "CL", False)
+    fill(T.ONE[:], 160, 1, "ONE")
     sel(T.Sh[:], T.ONE[:], [[-1, 160]], A_.is_equal, 16, 1, "ONE", "Sh")
-    iota(T.CL[:], [[8, 2], [1, 8], [16, 2]], 0, 0, "CL")
-    iota(T.DGi[:], [[-1, 256]], 256, 1, "DGi")
+    iota(T.K16[:], [[16, 16]], 0, 0, "K16")
     sel(T.BO[:], T.ONE[:, 0:128], [[-16, 8], [0, 16]], A_.is_ge, 0, 1, "ONE", "BO")
-    iota(T.PAY[:], [[-1, 256]], 256, 0, "PAY", True)
     sel(T.BO[:], T.BO[:], [[16, 8], [0, 16]], A_.is_ge, 15, -1, "BO", "BO")
-    iota(T.BL[:], [[1, 16], [16, 16]], 0, 0, "BL")
-    iota(T.C16[:], [[16, 16]], 0, 0, "C16", True)
-    iota(T.OPP[:], [[2, 1544], [-1, 2]], 1, 0, "OPP", True)
+    iota(T.PAY[:], [[-1, 256]], 256, 0, "PAY")
+    iota(T.OPP[:, 1536:3088], [[2, 776], [-1, 2]], 1537, 0, "OPP1")
+    fill(T.NEG[:], 256, -2048, "NEG")
+    fill(T.TH[:, :, 0], 16, -BIG, "THp")
     idb = T.Sh[:, 16:144]
-    r16, m1, m0, colr, colE, b15, colD, n0, n1 = [T.col[:, k:k + 1] for k in range(9)]
+    r16, m1, k0, k1, colr, b15, colD, n0, n1, r16x = [T.col[:, k:k + 1] for k in range(10)]
 
     memset(T.RM[:], 1.0, "RM")
-    memset(T.OV[:, 0:256], 1.0, "OV")
+    memset(T.OV[:], 1.0, "OV")
     ts(T.PLa[:], T.PL[:], 255, A_.bitwise_and, "PL", "PLa")
     ts(T.f4[:, 0:1], T.PL[:, 0:1], 8, A_.arith_shift_right, "PL", "f4", 1, A_.bitwise_and)
-    memset(T.th0[:], 0.5, "th0")
-    memset(T.th1[:], 0.0, "th1")
+    ts(T.Kf[:], T.PL[:], 4, A_.arith_shift_right, "PL", "Kf", 15, A_.bitwise_and)
+    memset(T.RM[:, 0::16], 0.0, "RM")
     copy(m1, T.f4[:, 0:1], "f4", "m1")
     copy(r16, T.PLa[:, 0:1], "PLa", "r16")
     copy(T.PLu[:], T.PLa[:], "PLa", "PLu")
-    ts(m0, m1, -1.0, A_.mult, "m1", "m0", 1.0, A_.add)
+    copy(T.rl[:], T.Kf[:], "Kf", "rl")
     ts(n1, m1, 2.0 ** -16, A_.mult, "m1", "n1")
     ts(n0, m1, -2.0 ** -16, A_.mult, "m1", "n0", 2.0 ** -16, A_.add)
     ts(b15, r16, -1.0 / 256, A_.mult, "r16", "b15", 15.0 / 16, A_.add)
-    memset(T.RM[:, 0::16], 0.0, "RM")
-    memset(T.th0[:, 0::16], 0.0, "th0")
-    memset(T.th1[:, 0::16], -2.0 ** 28, "th1")
-    memset(T.L[:, 3072:3088], 0.0, "Lp")
-    memset(T.OV[:, 256:272], 0.0, "OVp")
-    memset(T.E[:], 0.0, "E")
-    for x in (T.XT0, T.XT1):
-        memset(x[:, 256::CH], 0.0, x.name + "p")
-        memset(x[:, 257::CH], 0.0, x.name + "q")
-    scan(T.THR[:], T.th0[:], T.th1[:], A_.mult, A_.add, "th0 th1", "THR")
     copy(T.CLu[:], T.CL[:], "CL", "CLu")
     copy(T.capF[:], T.capI[:], "capI", "capF")
     ts(colr, r16, CH / 16.0, A_.mult, "r16", "colr", 256.0, A_.add)
-    ts(colE, r16, 16.0, A_.mult, "r16", "colE", 256.0, A_.add)
     turn(T.capT[:], T.capF[:], "capF", "capT")
+    memset(T.L[:, 3072:3088], 0.0, "Lp")
+    memset(T.E[:], 0.0, "E")
+    copy(T.Off[:, 0:256], T.A[:, 0:256].indirect(T.PLu[:, 0:16]), "A01 PLu", "Off0")
+    copy(T.Ap0[:], T.A[:, 0:256], "A01", "Ap0")
+    ts(T.D16[:], T.K16[:], r16, A_.is_equal, "K16 r16", "D16")
+    for x in (T.XT0, T.XT1):
+        memset(x[:, 256::CH], 0.0, x.name + "p")
+        memset(x[:, 257::CH], 0.0, x.name + "q")
+    ts(T.E[:, 15:143:16], T.BO[:, 0::16], 512.0, A_.mult, "BO", "E")
+    copy(T.Off[:, 256:512], T.A[:, 256:512].indirect(T.PLu[:, 0:16]), "A01 PLu", "Off1")
+    copy(T.Ap1[:], T.A[:, 256:512], "A01", "Ap1")
+    ts(k0, m1, -1.0, A_.add, "m1", "k0")
+    ts(k1, m1, -1.0, A_.mult, "m1", "k1")
+    ts(r16x, r16, -1.0, A_.mult, "r16", "r16x", 240.0, A_.add)
     ts(colD, r16, 1.0 / 16, A_.mult, "r16", "colD", 3841.0, A_.add)
     memset(T.BK[:, 1536:1544], 0, "BKp")
-    memset(T.DG[:, 256:272], 0.0, "DGp")
-    memset(T.EQ[:, 4096:4112], 0.0, "EQp")
-    ts(T.DGi[:], T.DGi[:], 15, A_.bitwise_and, "DGi", "DGi")
-    copy(T.Off[:, 0:256], T.A[:, 256:512].indirect(T.PLu[:, 0:16]), "A0 PLu", "Off0")
-    copy(T.Af0[:], T.A[:, 256:512], "A0", "Af0")
-    ts(T.DG[:, 0:256], T.DGi[:], 0.0, A_.is_equal, "DGi", "DG")
-    ts(T.E[:, 15:143:16], T.BO[:, 0::16], 512.0, A_.mult, "BO", "E")
-    copy(T.Off[:, 256:512], T.A[:, 512:768].indirect(T.PLu[:, 0:16]), "A1 PLu", "Off1")
-    tt(T.pw[:], T.THR[:, 0:16], T.DG[:, 0:16], A_.mult, "THR DG", "pw")
-    copy(T.Af1[:], T.A[:, 512:768], "A1", "Af1")
-    scan(T.pm[:], T.pw[:], T.pw[:], A_.min, A_.min, "pw", "pm")
-    act(T.B15[:], idb, "Sh b15", "B15", b15)
-    act(T.W0f[:], T.Sh[:], "Sh n0", "W0f", n0)
-    act(T.W1f[:], T.Sh[:], "Sh n1", "W1f", n1)
-    act(T.idf[:], idb, "Sh", "idf")
-    act(T.I4[:], idb, "Sh", "I4", 4096.0)
-    act(T.In[:], idb, "Sh", "In", -2.0)
+    memset(T.h17[:, :, 0], 2000.0, "h17p")
+    ts(T.DR[:], T.K16[:], r16x, A_.is_equal, "K16 r16x", "DR")
+    copy(T.BOh[:], T.BO[:], "BO", "BOh")
+    memset(T.Tab[:, :, 0:15], 0.0, "Tab0")
+    ts(T.Tab[:, :, 16:32], T.BO[:], -2.0 ** 17, A_.mult, "BO", "Tab1")
+    ts(T.Tab[:, :, 15], T.BO[:, 0::16], 4096.0, A_.mult, "BO", "Tab2")
+    for j in range(16):
+        copy(T.WJ[:, 128 * j:128 * j + 128], T.Tab[:, :, 15 - j:31 - j], "Tab0 Tab1 Tab2", "WJ.%d" % j)
+    for k in (96, 192, 384, 768):
+        act(T.OPP[:, k:2 * k], T.OPP[:, 0:k], "OPP0", "OPP0", 1.0, float(k))
 
     def capital(t):
         act(T["C%d" % t][:], T.capT[:, 0:32].indirect(T.CLu[:, 16 * t:16 * t + 16]), "capT CLu", "C%d" % t, -512.0, -512.0)
@@ -235,24 +237,25 @@ def rank_program(g, core, T, topo):
     def swap(t, w0, w1, src, names, stop):
         ak = T["AK%d" % t]
         for u, be, l in ((0, 0, w0[:, 16:144]), (0, 1, w0[:, 0:128]), (1, 1, w1[:, 16:144]), (1, 0, w1[:, 32:160])):
-            mm(ak[:, 0:8, u, :], l, src[:, :, be, :], False, stop and u == 1 and be == 0, names, "@AK%d" % t)
+            mm(ak[:, 0:8, 16 * u:16 * u + 16], l, src[:, :, be, :], False, stop and u == 1 and be == 0, names, "@AK%d" % t)
 
     def ak_open(t):
-        mm(T["AK%d" % t][:, 0:8, :, :], T.B15[:], T.OV[:, 0:256], True, False, "B15 OV", "@AK%d" % t)
-        swap(t, T.W0f, T.W1f, T["Af%d" % t], "W0f W1f Af%d" % t, t == 0)
+        mm(T["AK%d" % t][:, 0:8, :], T.B15[:], T.OV[:], True, False, "B15 OV", "@AK%d" % t)
+        swap(t, T.W0f, T.W1f, T["Ap%d" % t], "W0f W1f Ap%d" % t, t == 0)
 
     def x_gather(q, t, r0, r1):
         src = T.L[:, 0:3088].indirect(T.Off[:, 256 * t + 16 * r0:256 * t + 16 * r1])
         dst = T["X%d" % t][:, 256 * r0:256 * r1]
         (copy if q == "V" else act)(dst, src, "L Lp Off%d" % t, " ".join("X%d.%d" % (t, r) for r in range(r0, r1)))
 
-    def x_turn(t, r):
-        xt = T["XT%d" % t][:, CH * r:CH * r + 256]
-        turn(xt, T["X%d" % t][:, 256 * r:256 * r + 256], "X%d.%d" % (t, r), "XT%d.%d" % (t, r))
-        mm(T["Z%d" % t][:, 0:256], T.E[:, 15 - r:143 - r], xt, False, r == 15, "E XT%d.%d" % (t, r), "@Z%d" % t)
+    def x_turn(t, rs, last=None):
+        for r in rs:
+            xt = T["XT%d" % t][:, CH * r:CH * r + 256]
+            turn(xt, T["X%d" % t][:, 256 * r:256 * r + 256], "X%d.%d" % (t, r), "XT%d.%d" % (t, r))
+            mm(T["Z%d" % t][:, 0:256], T.E[:, 15 - r:143 - r], xt, False, r == last, "E XT%d.%d" % (t, r), "@Z%d" % t)
 
     def ak_out(t):
-        act(T.AKs[:], T["AK%d" % t][:, 0:8, :, :], "@AK%d" % t, "AKs")
+        act(T.AKs[:], T["AK%d" % t][:, 0:8, :], "@AK%d" % t, "AKs")
 
     def offers(t, z, zname):
         xt = " ".join("XT%d.%d" % (t, r) for r in range(16)) + " XT%dp XT%dq" % (t, t)
@@ -264,179 +267,200 @@ def rank_program(g, core, T, topo):
         turn(T.K2b[:], T.K2a[:], "K2a", "K2b")
         segmax(T.K2[:], T.K2b[:], "K2b", "K2")
         ts(T.KI[:], T.K2[:, 15::16], 65536.0, A_.mult, "K2", "KI", float(FLOOR), A_.max)
-        ts(T.M32[:, :, 0, :], T.KI[:], 4095, A_.bitwise_and, "KI", "Me")
-        ts(T.M32[:, :, 1, :], T.KI[:], 1, A_.arith_shift_right, "KI", "Mc", 2047, A_.bitwise_and)
+        ts(T.M32[:, 0::3, :], T.KI[:], 4095, A_.bitwise_and, "KI", "Me")
+        ts(T.M32[:, 1:3, :], T.KI[:], 1, A_.arith_shift_right, "KI", "Mc", 2047, A_.bitwise_and)
         copy(T["MU%d" % t][:], T.M32[:], "Me Mc", "MU%d" % t)
         send(T["MU%d" % t], T["R%d" % t], 16, [rank + 1 + 2 * t, rank + 2 + 2 * t], "arr%d" % t, "MU%d" % t)
 
     def offered():
         ts(T.f4[:], T.KI[:], 12, A_.arith_shift_right, "KI", "f4", 15, A_.bitwise_and)
-        ts(T.t4[:], T.KI[:], 65536.0, A_.is_lt, "KI", "t4", 256.0, A_.mult)
-        tt(T.v4[:], T.t4[:], T.f4[:], A_.subtract, "t4 f4", "v4")
-        ts(T.pio[:], T.v4[:], 15.0, A_.add, "v4", "pio")
+        copy(T.pio[:], T.f4[:], "f4", "pio")
 
-    def offered_rows(t):
-        sc, bi = ((1.0, -1.0), (-2.0, 4.0))[t]
-        act(T["OH%d" % t][:], T.DG[:, 0:272].indirect(T.pio[:, 0:16]), "DG DGp pio", "OH%d" % t, sc, bi)
-        act(T["OV%d" % t][:], T.OV[:, 0:272].indirect(T.pio[:, 0:16]), "OV OVp pio", "OV%d" % t, 1.0, 0.5)
+    def place_row(t):
+        sc, bi = ((float(NONE), -24576.0), (0.5, -3.5))[t]
+        act(T["OH%d" % t][:], T.DR[:, 0:16].indirect(T.pio[:, 0:16]), "DR pio", "OH%d" % t, sc, bi)
 
-    eq_all = " ".join("EQ.%d" % r for r in range(16)) + " EQp"
-    a_all = "Ad A0 A1 A2"
+    def offer_row(t):
+        act(T["OV%d" % t][:], T.OPP[:, 0:3088].indirect(T["MU%d" % t][:, 8:24]), "OPP0 OPP1 MU%d" % t, "OV%d" % t,
+            -1.0, 1537.0, SIGN)
+
+    af_all = "Afd Af0 Af1 Af2"
     lf_all = "LFd LF0 LF1 LF2 LF3"
+    EBs = T.EB[:, 0:256]
 
-    def holders(t):
-        R = T["R%d" % t]
-        rn = "R%d" % t
-        mm(T.HR[:, 0:256], T.I4[:], T.DG[:, 0:256], True, False, "I4 DG", "@HR")
-        mm(T.G[:, 0:256], T.In[:], T.THR[:], True, False, "In THR", "@G")
+    def candidates(t):
+        R, rn = T["R%d" % t], "R%d" % t
+        mm(T.SC[:, 0:256], idb, T.NEG[:], True, False, "Sh NEG", "@SC")
+        mm(T.HR[:, 0:256], idb, T.DGc[:], True, False, "Sh DGc", "@HR")
+        mm(T.AK0[:, :, 0:16], idb, T.DGc[:], True, False, "Sh DGc", "@AK0")
+        mm(T.G[:, 0:272], idb, T.TH[:], True, False, "Sh TH THp", "@G")
+        copy(T.cP[:], T.BK[:, 0:1544].indirect(R[:, 8:24]), "BK BKp " + rn, "cP")
         for b in range(2):
-            ts(T.cF[:, 128 * b:128 * b + 128], T.BK[:, 0:1544].indirect(R[:, 16 * b + 8:16 * b + 16]), 1.0, A_.add,
-               "BK BKp " + rn, "cF%d" % b)
-            act(T.Eb[:, 128 * b:128 * b + 128], T.OPP[:, 0:3088].indirect(R[:, 16 * b:16 * b + 8]), "OPP " + rn, "Eb%d" % b)
-        ts(T.cP[:], T.cF[:, 0:256].indirect(T.PLu[:, 0:16]), -1.0, A_.add, "cF0 cF1 PLu", "cP")
-        cuts = [0, 1, 2, 4, 6, 8, 10, 12, 14, 15, 16]
-        for r0, r1 in zip(cuts[:-1], cuts[1:]):
-            c0, c1 = 256 * r0, 256 * r1
-            act(T.IN1[:, c0:c1], T.Eb[:, 0:256].indirect(T.BLu[:, 16 * r0:16 * r1]), "Eb0 Eb1 BLu", "IN.%d" % r0)
-            tt(T.EQ[:, c0:c1], T.A[:, 256:2816].indirect(T.cP[:, 16 * r0:16 * r1]), T.IN1[:, c0:c1], A_.is_equal,
-               "A0 A1 A2 cP IN.%d" % r0, " ".join("EQ.%d" % r for r in range(r0, r1)))
-            for r in range(r0, r1):
-                mm(T.CNT[:, 0:256], T.E[:, 15 - r:143 - r], T.EQ[:, 256 * r:256 * r + 256], r == 0, r == 15,
-                   "E EQ.%d" % r, "@CNT")
+            act(T.Eb[:, 128 * b:128 * b + 128], T.OPP[:, 0:3088].indirect(R[:, 24 * b:24 * b + 8]), "OPP0 OPP1 " + rn,
+                "Eb%d" % b)
+        mm(EBs, T.idf[:], T.Eb[:], True, True, "idf Eb0 Eb1", "@EB")
+        for c0, c1 in ((0, OWN[t]), (OWN[t], 128), (128, 192), (192, 256)):
+            (act if c0 else copy)(T.RAW[:, 16 * c0:16 * c1], T.Af[:, 256:2816].indirect(T.cP[:, c0:c1]),
+                                  "Af0 Af1 Af2 cP", "RAW.%d" % (c1 // 128 * c1))
+        ts(T.c16[:], T.cP[:], -1279.0, A_.add, "cP", "c16")
+
+    def holders(c0, c1):
+        rd = "RAW.0 RAW.128" if c0 == 0 else "RAW.%d" % (c1 // 128 * c1)
+        for j in range(16):
+            eq = T.EQ[:, 256 * j + c0:256 * j + c1]
+            tt(eq, T.RAW[:, 16 * c0 + j:16 * c1:16], T.EB[:, c0:c1], A_.is_equal, rd + " @EB", "EQ.%d.%d" % (j, c0))
+            mm(T.SC[:, c0:c1], T.WJ[:, 128 * j:128 * j + 128], eq, False, c1 == 256 and j == 15,
+               "WJ.%d EQ.%d.%d" % (j, j, c0), "@SC")
 
     def first_holder():
-        tt(T.K3a[:], T.CNT[:, 0:256], T.PAY[:], A_.min, "@CNT PAY", "K3a")
-        segmax(T.K3[:], T.K3a[:], "K3a", "K3")
-        ts(T.jo[:], T.K3[:, 15::16], -1.0, A_.mult, "K3", "jo", 256.0, A_.add)
-        ts(T.EO[:], T.K3[:, 15::16], -1.0, A_.mult, "K3 colE", "EO", colE, A_.add)
-        tt(T.OHc[:], T.DG[:, 0:272].indirect(T.jo[:, 0:16]), T.cF[:], A_.mult, "DG DGp jo cF0 cF1", "OHc")
-        mm(T.HR[:, 0:256], T.BOf[:], T.OHc[:], False, True, "BOf OHc", "@HR")
+        tt(T.t32[:], T.SC[:, 0:256], T.c16[:], A_.min, "@SC c16", "t32")
+        ts(T.t16[:], T.t32[:], -1280.0, A_.max, "t32", "t16")
+        mm(T.HR[:, 0:256], T.BOh[:], T.t16[:], False, True, "BOh t16", "@HR")
+        mm(T.AK0[:, :, 0:16], T.BOh[:], T.t16[:], False, True, "BOh t16", "@AK0")
 
-    def compare():
-        tt(T.h16[:], T.HR[:, 0:256], T.DX[:], A_.subtract, "@HR DX", "h16")
+    def compare(t):
+        tt(T.h17[:, :, 1:17], T.HR[:, 0:256], T.DX[:], A_.subtract, "@HR DX", "h17")
         segmax(T.hc[:], T.HR[:, 0:256], "@HR", "hc")
-        act(T.NF[:], T.HR[:, 0:256], "@HR", "NF", -1.0, 1.0, RELU)
-        act(T.HD[:], T.HR[:, 0:256], "@HR", "HD")
+        act(T.NF[:, :, 1:17], T.AK0[:, :, 0:16], "@AK0", "NF", -1.0, 1.0, RELU)
+        act(T.HD[:], T.AK0[:, :, 0:17], "@AK0", "HD")
         for c in range(16):
-            lo = 16 * c
-            ts(T.EQ2[:, c, 0:256 - lo], T.h16[:, lo:256], 5376.0, A_.add, "h16 hc", "E2.%d" % c,
-               T.hc[:, lo + 15:lo + 16], A_.is_equal)
+            n = 17 * (16 - c)
+            ts(T.EQ2[:, c, 0:n], T.h17[:, c:16, :], 5376.0, A_.add, "h17 h17p hc", "E2.%d" % c,
+               T.hc[:, 16 * c + 15:16 * c + 16], A_.is_equal)
             if c == 0:
                 ts(T.HO[:], T.hc[:, 15::16], -3841.0, A_.add, "hc", "HO")
+                act(T.Acol[:], T.Af[:, 0:2816].indirect(T.HO[:, 0:16]), af_all + " HO", "Acol")
             if c < 15:
-                mm(T.G[:, lo + 16:256], T.LO[:], T.EQ2[:, c, 16:256 - lo], False, False, "LO E2.%d" % c, "@G")
+                mm(T.G[:, 17 + 17 * c:272], T.LO[:], T.EQ2[:, c, 17:n], False, False, "LO E2.%d" % c, "@G")
             if c == 11:
-                mm(T.G[:, 0:256], T.LO[:], T.NF[:], False, False, "LO NF", "@G")
-        mm(T.G[:, 0:256], T.LD[:], T.EQ2[:, :, 0:16], False, True, "LD " + " ".join("E2.%d" % c for c in range(16)), "@G")
+                mm(T.G[:, 0:272], T.LO[:], T.NF[:], False, False, "LO NF NFp", "@G")
+        mm(T.G[:, 0:272], T.LT[:], T.EQ2[:, :, 0:17], False, True, "LT " + " ".join("E2.%d" % c for c in range(16)), "@G")
+        tt(T.eqb[:], T.Acol[:], EBs, (A_.is_equal, A_.not_equal)[t], "Acol @EB", "eqb")
+
+    def columns():
+        scan(T.Fk[:], T.G[:, 0:272], T.HD[:], A_.min, A_.max, "@G HD", "Fk")
+        ts(T.SO[:], T.Fk[:, 16::17], -3841.0, A_.add, "Fk", "SO")
 
     def verdicts(t):
         ac = T["ac%d" % t]
-        tt(T.V1[:], T.G[:, 0:256], T.HD[:], A_.min, "@G HD", "V1")
-        act(ac[:], T.V1[:], "V1", "ac%d" % t, 1.0, 0.0, SIGN)
-        send(ac, T["AC%d" % t], 128, [rank - 1 - 2 * t, rank - 2 - 2 * t], "ack%d" % t, "ac%d" % t)
-        segmax(T.Fk[:], T.V1[:], "V1", "Fk")
-        tt(T.F2[:], T.Fk[:, 15::16], T.DM[:], A_.max, "Fk DM", "F2")
-        ts(T.SO[:], T.F2[:], -3841.0, A_.add, "F2", "SO")
+        act(ac[:], T.G[:, 0:272], "@G", "ac%d" % t, 1.0, 0.0, SIGN)
+        send(ac, T["AC%d" % t], 8, [rank - 1 - 2 * t, rank - 2 - 2 * t], "ack%d" % t, "ac%d" % t)
 
     def said(t, q):
-        sd, ps = T["sd%d" % t], T.AK0[:, 0:8, :, :]
-        mm(ps, idb, T["OV%d" % t][:], True, False, "Sh OV%d" % t, "@AK0")
-        mm(ps, T.Ih[:], T["AC%d" % t][:], False, True, "Ih AC%d" % t, "@AK0")
-        act(sd[:], ps, "@AK0", "sd%d" % t)
+        sd, ps = T["sd%d" % t], T.SC[:, 0:256]
+        mm(ps, idb, T["OV%d" % t][:], True, False, "Sh OV%d" % t, "@SC")
+        mm(ps, T.BOq[:], T["AC%d" % t][:, :, 1:17], False, True, "BOq AC%d" % t, "@SC")
+        act(sd[:], ps, "@SC", "sd%d" % t, 2.0, -8.0, RELU)
         dma(q, T.said[:, 256 * t:256 * t + 256], sd[0::16, :], "sd%d" % t, "out%d" % t, "o%d" % t)
 
     def left(lo, hi, rd, wr):
-        ts(T.LF[:, lo:hi], T.A[:, lo:hi], float(NONE), A_.is_lt, rd, wr)
+        act(T.LF[:, lo:hi], T.Af[:, lo:hi], rd, wr, -1.0, float(NONE), SIGN)
 
+    act(T.idf[:], idb, "Sh", "idf")
     capital(0)
-    capital(1)
+    act(T.B15[:], idb, "Sh b15", "B15", b15)
+    act(T.W0f[:], T.Sh[:], "Sh n0", "W0f", n0)
+    act(T.W1f[:], T.Sh[:], "Sh n1", "W1f", n1)
     ak_open(0)
     z_open(0)
-    act(T.DX[:], T.DG[:, 0:256], "DG", "DX", 4096.0, 1280.0)
+    act(T.DG[:], T.D16[:, 0:16].indirect(T.rl[:, 0:16]), "D16 rl", "DG")
+    capital(1)
     ak_out(0)
-    x_gather("V", 0, 0, 3)
-    x_gather("V", 0, 3, 6)
-    for r0, r1 in ((6, 8), (8, 10), (10, 12), (12, 14), (14, 15), (15, 16)):
+    act(T.AK0[:, :, 16], T.K16[:], "K16 colD", "@AK0", 1.0, colD)
+    act(T.Af[:, 256:512], T.Ap0[:], "Ap0", "Af0")
+    act(T.Af[:, 512:768], T.Ap1[:], "Ap1", "Af1")
+    act(T.DGc[:], T.DG[:], "DG", "DGc", 4096.0, 20480.0)
+    act(T.TH[:, :, 1:17], T.DG[:], "DG", "TH", 8192.0 - BIG, float(BIG))
+    x_gather("V", 0, 0, 2)
+    x_gather("S", 0, 6, 8)
+    x_turn(0, (0, 1))
+    x_gather("V", 0, 2, 4)
+    x_gather("S", 0, 8, 10)
+    x_turn(0, (2, 3, 6, 7))
+    x_gather("V", 0, 4, 6)
+    for r0, r1 in ((10, 12), (12, 14), (14, 15), (15, 16)):
         x_gather("S", 0, r0, r1)
-    for r in range(16):
-        x_turn(0, r)
-    for r0 in range(0, 10, 2):
-        x_gather("S", 1, r0, r0 + 2)
-    copy(T.BLu[:], T.BL[:], "BL", "BLu")
+    x_turn(0, (4, 5, 8, 9, 10, 11, 12, 13, 14, 15), 15)
+    for r0, r1 in ((0, 4), (4, 8), (8, 10)):
+        x_gather("S", 1, r0, r1)
     offers(0, T.Z0[:, 0:256], "@Z0")
     ak_open(1)
     z_open(1)
+    sel(T.LT[:], T.BO[:], [[1, 128]], A_.is_gt, 0, -1, "BO", "LT0")
+    fill(T.NF[:, :, 0], 16, 0, "NFp")
+    fill(T.Af[:, 0:256], 256, 0, "Afd")
+    fill(T.Y[:, 512:768], 256, 0, "Y")
+    fill(T.LF[:, 0:256], 256, 0, "LFd")
 
+    copy(T.Af[:, 768:2816], T.A[:, 512:2560], "A2", "Af2")
     offered()
-    memset(T.A[:, 0:256], 0, "Ad")
-    for r in range(10):
-        x_turn(1, r)
+    x_turn(1, range(0, 6))
 
-    holders(0)
-    act(T.BOf[:], T.BO[:], "BO", "BOf")
+    candidates(0)
+    x_turn(1, range(6, 10))
+    holders(0, 128)
+    copy(T.r32[:], T.R0[:], "R0", "r32")
+    ts(T.q1[:], T.r32[:, 1:3, :], 4.0, A_.mult, "r32", "q1", 1.0, A_.add)
+    holders(128, 192)
+    tt(T.q2[:], T.q1[:], T.r32[:, 0::3, :], A_.subtract, "q1 r32", "q2")
+    copy(T.oo[:], T.q2[:], "q2", "oo")
+    holders(192, 256)
+    act(T.DX[:], T.DG[:], "DG", "DX", 4096.0, 1280.0)
+    act(T.LO[:], T.BO[:], "BO", "LO", -2.0 ** 14)
     for r0 in (10, 12, 14):
         x_gather("S", 1, r0, r0 + 2)
-    act(T.LO[:], T.BO[:], "BO", "LO", -2.0 ** 29)
-    act(T.LD[:], T.BO[:], "BO pm", "LD", T.pm[:, 15:16])
-    copy(T.r32[:], T.R0[:], "R0", "r32")
-    ts(T.q1[:], T.r32[:, :, 1, :], 4.0, A_.mult, "r32", "q1", 1.0, A_.add)
-    tt(T.q2[:], T.q1[:], T.r32[:, :, 0, :], A_.subtract, "q1 r32", "q2")
+    act(T.LT[:], T.LT[:], "LT0", "LT", -2.0 ** 14)
     first_holder()
-    copy(T.oo[:], T.q2[:], "q2", "oo")
-    for r in range(10, 14):
-        x_turn(1, r)
-    eq = T.EQ[:, 0:4112].indirect(T.EO[:, 0:16])
-    act(T.eqf[:], eq, eq_all + " EO", "eqf", float(NONE))
-    compare()
-    act(T.eqb[:], eq, eq_all + " EO", "eqb")
+    x_turn(1, (10, 11))
+    compare(0)
     act(T.BO5[:], T.BO[:], "BO", "BO5", 512.0)
-    act(T.DM[:], T.C16[:], "C16 colD", "DM", 1.0, colD)
-    mm(T.CN[:, 0:256], T.BO5[:], T.eqb[:], True, True, "BO5 eqb", "@CN")
+    act(T.eqf[:], T.eqb[:], "eqb", "eqf", float(NONE))
+    mm(T.Z0[:, 0:256], T.BO5[:], T.eqb[:], True, True, "BO5 eqb", "@Z0")
     act(T.Lo[:], T.L[:, 0:3088].indirect(T.oo[:, 0:16]), "L Lp oo", "Lo")
-    act(T.Y[:, 512:768], T.OV[:, 0:256], "OV", "Y", 0.0)
-    act(T.cn[:], T.CN[:, 0:256], "@CN", "cn")
-    tt(T.nc[:], T.A[:, 0:2816].indirect(T.HO[:, 0:16]), T.eqf[:], A_.max, a_all + " HO eqf", "nc")
-    x_turn(1, 14)
-    verdicts(0)
-    act(T.W0b[:], T.Sh[:], "Sh m0", "W0b", m0)
-    act(T.W1b[:], T.Sh[:], "Sh m1", "W1b", m1)
-    act(T.I3[:], idb, "Sh", "I3", float(NONE))
-    act(T.Ih[:], idb, "Sh", "Ih", 0.5)
-    act(T.LF[:, 0:256], T.OV[:, 0:256], "OV", "LFd", 0.0)
-    x_turn(1, 15)
-    copy(T.A[:, 0:2816].indirect(T.SO[:, 0:16]), T.nc[:], "nc SO", a_all)
+    act(T.cn[:], T.Z0[:, 0:256], "@Z0", "cn")
+    act(T.W0b[:], T.Sh[:], "Sh k0", "W0b", k0)
+    act(T.W1b[:], T.Sh[:], "Sh k1", "W1b", k1)
+    columns()
+    tt(T.Af[:, 0:2816].indirect(T.SO[:, 0:16]), T.Acol[:], T.eqf[:], A_.max, "SO Acol eqf", af_all)
+    x_turn(1, (12, 13, 14, 15), 15)
     tt(T.Y[:, 0:2816].indirect(T.SO[:, 0:16]), T.Lo[:], T.cn[:], A_.mult, "SO Lo cn", "Y")
-    ts(T.Pen[:], T.A[:, 512:768], float(NONE), A_.is_equal, "A1", "Pen", -512.0, A_.mult)
-    offered_rows(0)
+    verdicts(0)
+    act(T.Pen[:], T.Af[:, 512:768], "Af1", "Pen", 512.0, -512.0 * (NONE - 1), RELU)
     swap(1, T.W0b, T.W1b, T.Pen, "W0b W1b Pen", True)
+    place_row(0)
     ak_out(1)
 
     turn(T.YT[:], T.Y[:, 512:768], "Y", "YT")
     tt(T.Zc[:], T.Z1[:, 0:256], T.YT[:], A_.subtract, "@Z1 YT", "Zc")
-    mm(T.Z0[:, 0:256], T.I3[:], T.OH0[:], True, False, "I3 OH0", "@Z0")
-    mm(T.Z0[:, 0:256], T.I3[:], T.AC0[:], False, True, "I3 AC0", "@Z0")
+    act(T.BOa[:], T.BO[:], "BO", "BOa", 1536.0)
+    act(T.BOq[:], T.BO[:], "BO", "BOq", 0.25)
+    offer_row(0)
+    mm(T.Z0[:, 0:256], idb, T.OH0[:], True, False, "Sh OH0", "@Z0")
+    mm(T.Z0[:, 0:256], T.BOa[:], T.AC0[:, :, 1:17], False, True, "BOa AC0", "@Z0")
+    left(512, 1792, "Af1 Af2", "LF1 LF2")
     said(0, "Y")
     offers(1, T.Zc[:], "Zc")
-    tt(T.A[:, 256:512], T.A[:, 256:512], T.Z0[:, 0:256], A_.max, "A0 @Z0", "A0")
+    tt(T.Af[:, 256:512], T.Af[:, 256:512], T.Z0[:, 0:256], A_.max, "Af0 @Z0", "Af0")
     offered()
-    offered_rows(1)
-    left(512, 1792, "A1 A2", "LF1")
 
-    holders(1)
-    left(256, 512, "A0", "LF0")
+    candidates(1)
+    for c0, c1 in ((0, 128), (128, 192), (192, 256)):
+        holders(c0, c1)
+    left(256, 512, "Af0", "LF0")
+    left(1792, 2816, "Af2", "LF3")
+    place_row(1)
     first_holder()
-    left(1792, 2304, "A2", "LF2")
-    act(T.eqb[:], eq, eq_all + " EO", "eqb", -1.0, 1.0)
-    compare()
-    left(2304, 2816, "A2", "LF3")
+    compare(1)
+    act(T.lc[:], T.Acol[:], "Acol", "lc", -1.0, float(NONE), SIGN)
+    offer_row(1)
     mm(T.Z0[:, 0:256], idb, T.OH1[:], True, False, "Sh OH1", "@Z0")
+    columns()
     verdicts(1)
-    act(T.lc[:], T.LF[:, 0:2816].indirect(T.HO[:, 0:16]), lf_all + " HO", "lc")
     tt(T.LF[:, 0:2816].indirect(T.SO[:, 0:16]), T.lc[:], T.eqb[:], A_.mult, "SO lc eqb", lf_all)
-    dma("Y", T.left[:, 512:2560], T.LF[:, 768:2816], "LF1 LF2 LF3", "out2", "o2")
+    dma("Y", T.left[:, 512:2560], T.LF[:, 768:2816], "LF2 LF3", "out2", "o2")
     dma("S", T.left[:, 0:256], T.LF[:, 256:512], "LF0", "out3", "o3")
-    mm(T.Z0[:, 0:256], T.In[:], T.AC1[:], False, True, "In AC1", "@Z0")
-    tt(T.LG[:], T.LF[:, 512:768], T.Z0[:, 0:256], A_.min, "LF1 @Z0", "LG")
+    mm(T.Z0[:, 0:256], T.BOq[:], T.AC1[:, :, 1:17], False, True, "BOq AC1", "@Z0")
+    tt(T.LG[:], T.LF[:, 512:768], T.Z0[:, 0:256], A_.is_gt, "LF1 @Z0", "LG")
     dma("Y", T.left[:, 256:512], T.LG[:], "LG", "out4", "o4")
     said(1, "S")
     add("Y", None, "out0 out1 out2 out3 out4", "")

@@ -6,30 +6,38 @@ N = 8
 CH = 258
 NONE = 3072
 FLOOR = 15 * 4096 + NONE
-BIG = 2 ** 23
-OWN = (56, 72)
+UN = 2.0 ** -11
+OWN = (24, 40)
+CUTS = ((96, 160, 216, 256), (80, 128, 176, 224, 256))
+SUMS = CUTS
+SP = 128
+EARLY = (0, 128)
+GAP = 0
+REP = ((2, 2), (2, 2))
+STEP = (1, 1)
+TURN = 6
 
 _SB = {
-    B: "L:3088 ONE:160 Sh:160 W0b:160 W1b:160 B15:128 BO:128 BO5:128 BOa:128 BOq:128 LO:128 LT:128 E:144 D16:16 DR:16 "
-       "DG:256 DGc:256 DX:256 NEG:256 PAY:256 RM:256 OV:256 TH:16,17 Tab:8,32 WJ:2048 X0:4096 X1:4096 XT0:4128 XT1:4128 "
-       "OH0:256 OH1:256 OV0:256 OV1:256 EQ:4096 NF:16,17 EQ2:16,272 ac0:16,17 ac1:16,17 AC0:16,17 AC1:16,17 eqb:256 "
+    B: "L:3088 Sh:160 C128:160 W0b:160 W1b:160 B15:128 BO:128 BOa:128 LT:128 E:144 DR:16 D16:256 RT:272 "
+       "NV:256 PAY:256 RM:256 OV:256 Ut:256 WJ:2048 X0:4096 X1:4096 XT0:4128 XT1:4128 "
+       "OH0:256 OH1:256 OV0:256 OV1:256 EQ:4096 NF:16,17 EQ2:16,272 ac0:16,17 ac1:16,17 AC0:16,17 AC1:16,17 neb:256 "
        "Pen:8,2,16 LF:2816 lc:256 LG:256",
-    F: "capF:32 capT:32 col:12 idf:128 W0f:160 W1f:160 K16:16 OPP:3088 C0:256 C1:256 Af:2816 Ap0:8,2,16 Ap1:8,2,16 "
-       "AKs:256 K1:256 K2a:256 K2b:256 K2:256 Eb:256 RAW:4096 t32:256 hc:256 HD:272 Fk:272 Acol:256 eqf:256 cn:256 "
+    F: "capF:32 capT:32 Cs:32 col:4 PLf:16 idf:128 W0f:160 W1f:160 K16:16 OPP:3088 Af:2816 Ap:16,2,16 "
+       "AKs:256 K1:256 K2a:256 K2b:256 K2:256 Eb:256 RAW:4096 t32:256 hc:256 HD:272 Fk:272 Acol:256 nef:256 BOf:128 cn:256 "
        "r32:4,8 q1:16 q2:16 Lo:256 Y:2816 YT:256 Zc:256 sd0:256 sd1:256",
-    I: "A:2560 BK:1544 capI:32 PL:16 PLa:16 CL:32 Ki:16 Kf:16 KI:16 M32:4,8 f4:16",
-    U: "PLu:16 CLu:32 rl:16 Off:512 o1:16 MU0:32 MU1:32 R0:32 R1:32 pio:16 cP:256 HO:16 SO:16 oo:16",
-    H: "h17:16,17 c16:256 t16:256 BOh:128",
+    I: "A:2560 BK:1544 capI:32 PL:16 PLa:16 Ki:16 Kf:16 KI:16 M32:4,8 f4:16",
+    U: "PLu:16 Off:512 o1:16 MU0:32 MU1:32 R0:32 R1:32 pio:16 cP:256 HO:16 SO:16 oo:16",
+    H: "h17:16,17 c16:256 t16:256",
 }
 SCRATCH = {e.split(":")[0]: ("sbuf", [128] + [int(x) for x in e.split(":")[1].split(",")], dt)
            for dt, names in _SB.items() for e in names.split()}
 SCRATCH.update({k: ("psum", [128, 512], F) for k in ("Z0", "Z1", "SC", "HR", "G", "EB")})
 SCRATCH.update({k: ("psum", [128, 16, 32], F) for k in ("AK0", "AK1")})
-DMAS = ["dA0", "dL", "dcap", "dA2", "dBK", "o0", "o1", "o2", "o3", "o4"]
+DMAS = ["dA0", "dL", "dcap", "dA2", "dA3", "dBK", "dAf", "dWJ", "o0", "o1", "o2", "o3", "o4"]
 SEMAPHORES = ["cV", "cS", "cP", "cG", "sent", "arr0", "arr1", "ack0", "ack1"] + DMAS
 
 
-def _emit(ops, queues, T):
+def _emit(ops, queues, T, arrivals):
     writer, readers, bank = {}, {}, {}
     known = {q: set() for q in queues}
     snap, waits, needed = [], [], set()
@@ -63,11 +71,11 @@ def _emit(ops, queues, T):
             earlier[q].append(n)
             snap.append(known[q] | set(earlier[q]))
         else:
-            snap.append(known[q] | {n})
+            snap.append(known[q] | {m for m, o in enumerate(ops) if o[4] == sem})
     count, at = {q: 0 for q in queues}, {}
     for n, (q, fn, rd, wr, sem) in enumerate(ops):
         if sem is not None:
-            at[n] = (sem, 16)
+            at[n] = (sem, arrivals.get(sem, 16) * sum(1 for o in ops if o[4] == sem))
         elif n in needed:
             count[q] += 1
             at[n] = ("c" + q, count[q])
@@ -92,7 +100,7 @@ def rank_program(g, core, T, topo):
     A_ = AluOpType
     ID, RELU, SIGN = ActivationFunctionType.Identity, ActivationFunctionType.Relu, ActivationFunctionType.Sign
     V, S, P = g.vector, g.scalar, g.tensor
-    ops = []
+    ops, engines = [], {}
 
     def add(q, fn, rd, wr, sem=None):
         ops.append((q, fn, rd.split(), wr.split(), sem))
@@ -127,27 +135,28 @@ def rank_program(g, core, T, topo):
     def mm(o, l, r, start, stop, rd, wr):
         add("P", lambda: P.matmul(o, l, r, start, stop), rd, wr)
 
-    def iota(o, pat, base, cm, wr, small=True):
+    def iota(o, pat, base, cm, rd, wr, small=True):
         if small:
-            add("G", lambda: g.iota(o, pat, base, cm, allow_small_or_imprecise_dtypes=True), "", wr)
+            add("G", lambda: g.iota(o, pat, base, cm, allow_small_or_imprecise_dtypes=True), rd, wr)
         else:
-            add("G", lambda: g.iota(o, pat, base, cm), "", wr)
+            add("G", lambda: g.iota(o, pat, base, cm), rd, wr)
 
     def fill(o, n, c, wr):
-        iota(o, [[0, n]], c, 0, wr)
+        iota(o, [[0, n]], c, 0, "", wr)
 
-    def sel(o, i, pat, cmp, base, cm, rd, wr):
-        add("G", lambda: g.affine_select(o, i, pat, cmp, 0.0, base, cm), rd, wr)
+    def sel(o, i, pat, cmp, base, cm, rd, wr, other=0.0):
+        add("G", lambda: g.affine_select(o, i, pat, cmp, other, base, cm), rd, wr)
 
     def dma(q, o, i, rd, wr, sem):
         add(q, lambda: (g.sync if q == "Y" else g.scalar).dma_start(o, i), rd, wr, sem)
 
-    def send(src, dst, width, peers, sem, rd):
+    def send(src, dst, width, peers, sem, rd, step=1):
         trs = []
         for b, peer in enumerate(peers):
             c = T.cores[peer % N]
             eng = topo.engines(core, c)
-            half = eng[b * len(eng) // 2:(b + 1) * len(eng) // 2]
+            half = eng[b * len(eng) // 2:(b + 1) * len(eng) // 2:step]
+            engines[sem] = engines.get(sem, 0) + len(half)
             rid, pid = topo.addr(c)[:2]
             trs.append(RemoteDMATransfer(dst_ids=[DstId(rid=rid, pnc=pid)], dma_engine_mask=sum(1 << e for e in half),
                                          remote_sem=T.sem[sem], src=src[:, b * width:(b + 1) * width],
@@ -164,182 +173,214 @@ def rank_program(g, core, T, topo):
     dma("Y", T.A[:, 0:512], T.acct[:, 0:512], "", "A01 go", "dA0")
     dma("S", T.capI[:], T.cap[:, :], "", "capI", "dcap")
     dma("Y", T.L[:, 0:3072], T.loss[:, :], "", "L", "dL")
-    dma("Y", T.A[:, 512:2560], T.acct[:, 512:2560], "go", "A2", "dA2")
+    dma("Y", T.A[:, 512:1536], T.acct[:, 512:1536], "go", "A2.0", "dA2")
+    dma("Y", T.A[:, 1536:2560], T.acct[:, 1536:2560], "", "A2.1", "dA3")
     dma("Y", T.BK[:, 0:1536], T.book[:, :], "", "BK", "dBK")
 
-    iota(T.PL[:], [[1, 16]], 0, 16, "PL", False)
-    iota(T.OPP[:, 0:96], [[2, 48], [-1, 2]], 1, 0, "OPP0")
-    iota(T.CL[:], [[8, 2], [1, 8], [16, 2]], 0, 0, "CL", False)
-    fill(T.ONE[:], 160, 1, "ONE")
-    sel(T.Sh[:], T.ONE[:], [[-1, 160]], A_.is_equal, 16, 1, "ONE", "Sh")
-    iota(T.K16[:], [[16, 16]], 0, 0, "K16")
-    sel(T.BO[:], T.ONE[:, 0:128], [[-16, 8], [0, 16]], A_.is_ge, 0, 1, "ONE", "BO")
-    sel(T.BO[:], T.BO[:], [[16, 8], [0, 16]], A_.is_ge, 15, -1, "BO", "BO")
-    iota(T.PAY[:], [[-1, 256]], 256, 0, "PAY")
-    iota(T.OPP[:, 1536:3088], [[2, 776], [-1, 2]], 1537, 0, "OPP1")
-    fill(T.NEG[:], 256, -2048, "NEG")
-    fill(T.TH[:, :, 0], 16, -BIG, "THp")
     idb = T.Sh[:, 16:144]
-    r16, m1, k0, k1, colr, b15, colD, n0, n1, r16x = [T.col[:, k:k + 1] for k in range(10)]
+    colr, b15, n0, n1 = [T.col[:, k:k + 1] for k in range(4)]
+    memset(T.OV[:], 1.0, "OV")
+    memset(T.Ut[:], 0.0, "Ut")
+    iota(T.PL[:], [[1, 16]], 0, 16, "", "PL", False)
+    iota(T.OPP[:, 0:96], [[2, 48], [-1, 2]], 1, 0, "", "OPP0")
+    sel(T.Sh[:], T.OV[:, 0:160], [[-1, 160]], A_.is_equal, 16, 1, "OV", "Sh")
+    sel(T.BO[:], T.OV[:, 0:128], [[-16, 8], [0, 16]], A_.is_ge, 0, 1, "OV", "BO")
+    sel(T.BO[:], T.BO[:], [[16, 8], [0, 16]], A_.is_ge, 15, -1, "BO", "BO")
+    iota(T.PAY[:], [[-1, 256]], 256, 0, "", "PAY")
+    iota(T.Ut[0:16, :], [[-64, 16], [64, 16]], 2, 0, "", "Ut")
+    sel(T.Ut[0:16, :], T.Ut[0:16, :], [[1, 16], [-1, 16]], A_.is_ge, 0, 0, "Ut", "Ut")
+    for x in (256, 257):
+        fill(T.XT0[:, x::CH], 16, 0, "XT0.p%d" % x)
+    iota(T.OPP[:, 1536:3088], [[2, 776], [-1, 2]], 1537, 0, "", "OPP1")
 
     memset(T.RM[:], 1.0, "RM")
-    memset(T.OV[:], 1.0, "OV")
     ts(T.PLa[:], T.PL[:], 255, A_.bitwise_and, "PL", "PLa")
     ts(T.f4[:, 0:1], T.PL[:, 0:1], 8, A_.arith_shift_right, "PL", "f4", 1, A_.bitwise_and)
-    ts(T.Kf[:], T.PL[:], 4, A_.arith_shift_right, "PL", "Kf", 15, A_.bitwise_and)
     memset(T.RM[:, 0::16], 0.0, "RM")
-    copy(m1, T.f4[:, 0:1], "f4", "m1")
-    copy(r16, T.PLa[:, 0:1], "PLa", "r16")
     copy(T.PLu[:], T.PLa[:], "PLa", "PLu")
-    copy(T.rl[:], T.Kf[:], "Kf", "rl")
-    ts(n1, m1, 2.0 ** -16, A_.mult, "m1", "n1")
-    ts(n0, m1, -2.0 ** -16, A_.mult, "m1", "n0", 2.0 ** -16, A_.add)
-    ts(b15, r16, -1.0 / 256, A_.mult, "r16", "b15", 15.0 / 16, A_.add)
-    copy(T.CLu[:], T.CL[:], "CL", "CLu")
+    ts(n1, T.f4[:, 0:1], -2.0 ** -16, A_.mult, "f4", "n1")
+    ts(n0, T.f4[:, 0:1], 2.0 ** -16, A_.mult, "f4", "n0", -2.0 ** -16, A_.add)
+    ts(b15, T.PLa[:, 0:1], -1.0 / 256, A_.mult, "PLa", "b15", 15.0 / 16 + NONE / 65536, A_.add)
     copy(T.capF[:], T.capI[:], "capI", "capF")
-    ts(colr, r16, CH / 16.0, A_.mult, "r16", "colr", 256.0, A_.add)
-    turn(T.capT[:], T.capF[:], "capF", "capT")
     memset(T.L[:, 3072:3088], 0.0, "Lp")
+    turn(T.capT[:], T.capF[:], "capF", "capT")
     memset(T.E[:], 0.0, "E")
+    copy(T.PLf[:], T.PLa[:], "PLa", "PLf")
     copy(T.Off[:, 0:256], T.A[:, 0:256].indirect(T.PLu[:, 0:16]), "A01 PLu", "Off0")
-    copy(T.Ap0[:], T.A[:, 0:256], "A01", "Ap0")
-    ts(T.D16[:], T.K16[:], r16, A_.is_equal, "K16 r16", "D16")
-    for x in (T.XT0, T.XT1):
-        memset(x[:, 256::CH], 0.0, x.name + "p")
-        memset(x[:, 257::CH], 0.0, x.name + "q")
-    ts(T.E[:, 15:143:16], T.BO[:, 0::16], 512.0, A_.mult, "BO", "E")
+    ts(T.Ap[:], T.A[:, 0:512], -1.0, A_.mult, "A01", "Ap", float(NONE), A_.add)
     copy(T.Off[:, 256:512], T.A[:, 256:512].indirect(T.PLu[:, 0:16]), "A01 PLu", "Off1")
-    copy(T.Ap1[:], T.A[:, 256:512], "A01", "Ap1")
-    ts(k0, m1, -1.0, A_.add, "m1", "k0")
-    ts(k1, m1, -1.0, A_.mult, "m1", "k1")
-    ts(r16x, r16, -1.0, A_.mult, "r16", "r16x", 240.0, A_.add)
-    ts(colD, r16, 1.0 / 16, A_.mult, "r16", "colD", 3841.0, A_.add)
-    memset(T.BK[:, 1536:1544], 0, "BKp")
-    memset(T.h17[:, :, 0], 2000.0, "h17p")
-    ts(T.DR[:], T.K16[:], r16x, A_.is_equal, "K16 r16x", "DR")
-    copy(T.BOh[:], T.BO[:], "BO", "BOh")
-    memset(T.Tab[:, :, 0:15], 0.0, "Tab0")
-    ts(T.Tab[:, :, 16:32], T.BO[:], -2.0 ** 17, A_.mult, "BO", "Tab1")
-    ts(T.Tab[:, :, 15], T.BO[:, 0::16], 4096.0, A_.mult, "BO", "Tab2")
-    for j in range(16):
-        copy(T.WJ[:, 128 * j:128 * j + 128], T.Tab[:, :, 15 - j:31 - j], "Tab0 Tab1 Tab2", "WJ.%d" % j)
-    for k in (96, 192, 384, 768):
+    ts(T.E[:, 15:143:16], T.BO[:, 0::16], 512.0, A_.mult, "BO", "E")
+    for k in (96, 192):
         act(T.OPP[:, k:2 * k], T.OPP[:, 0:k], "OPP0", "OPP0", 1.0, float(k))
-
-    def capital(t):
-        act(T["C%d" % t][:], T.capT[:, 0:32].indirect(T.CLu[:, 16 * t:16 * t + 16]), "capT CLu", "C%d" % t, -512.0, -512.0)
-
-    def z_open(t):
-        z = T["Z%d" % t][:, 0:256]
-        mm(z, T.idf[:], T["C%d" % t][:], True, False, "idf C%d" % t, "@Z%d" % t)
-        mm(z, idb, T.PAY[:], False, False, "Sh PAY", "@Z%d" % t)
+    act(T.B15[:], idb, "Sh b15", "B15", b15)
+    act(T.W0f[:], T.Sh[:], "Sh n0", "W0f", n0)
+    act(T.W1f[:], T.Sh[:], "Sh n1", "W1f", n1)
+    for k in (384, 768):
+        act(T.OPP[:, k:2 * k], T.OPP[:, 0:k], "OPP0", "OPP0", 1.0, float(k))
+    dma("Y", T.Af[:, 256:768], T.Ap[:], "Ap", "Af0 Af1", "dAf")
+    for k in range(8):
+        dma("Y", T.WJ[16 * k:128, 256 * k:256 * k + 256], T.Ut[0:128 - 16 * k, :], "Ut", "WJ.%d" % k, "dWJ")
+        if k:
+            dma("Y", T.WJ[0:16 * k, 256 * k:256 * k + 256], T.Ut[16:16 + 16 * k, :], "Ut", "WJ0.%d" % k, "dWJ")
 
     def swap(t, w0, w1, src, names, stop):
         ak = T["AK%d" % t]
         for u, be, l in ((0, 0, w0[:, 16:144]), (0, 1, w0[:, 0:128]), (1, 1, w1[:, 16:144]), (1, 0, w1[:, 32:160])):
-            mm(ak[:, 0:8, 16 * u:16 * u + 16], l, src[:, :, be, :], False, stop and u == 1 and be == 0, names, "@AK%d" % t)
+            mm(ak[:, 0:8, 16 * u:16 * u + 16], l, src(be), False, stop and u == 1 and be == 0, names, "@AK%d" % t)
 
     def ak_open(t):
         mm(T["AK%d" % t][:, 0:8, :], T.B15[:], T.OV[:], True, False, "B15 OV", "@AK%d" % t)
-        swap(t, T.W0f, T.W1f, T["Ap%d" % t], "W0f W1f Ap%d" % t, t == 0)
+        swap(t, T.W0f, T.W1f, lambda be: T.Ap[:, 8 * t:8 * t + 8, be, :], "W0f W1f Ap", t == 0)
+
+    def z_open(t):
+        mm(T["Z%d" % t][:, 0:256], idb, T.PAY[:], True, False, "Sh PAY", "@Z%d" % t)
 
     def x_gather(q, t, r0, r1):
-        src = T.L[:, 0:3088].indirect(T.Off[:, 256 * t + 16 * r0:256 * t + 16 * r1])
-        dst = T["X%d" % t][:, 256 * r0:256 * r1]
-        (copy if q == "V" else act)(dst, src, "L Lp Off%d" % t, " ".join("X%d.%d" % (t, r) for r in range(r0, r1)))
+        h0, h1 = int(2 * r0), int(2 * r1)
+        src = T.L[:, 0:3088].indirect(T.Off[:, 256 * t + 8 * h0:256 * t + 8 * h1])
+        dst = T["X%d" % t][:, 128 * h0:128 * h1]
+        if h1 > h0:
+            (copy if q == "V" else act)(dst, src, "L Lp Off%d" % t, " ".join("X%d.%d" % (t, h) for h in range(h0, h1)))
 
-    def x_turn(t, rs, last=None):
+    def x_sum(t, rs, last=None):
         for r in rs:
-            xt = T["XT%d" % t][:, CH * r:CH * r + 256]
-            turn(xt, T["X%d" % t][:, 256 * r:256 * r + 256], "X%d.%d" % (t, r), "XT%d.%d" % (t, r))
-            mm(T["Z%d" % t][:, 0:256], T.E[:, 15 - r:143 - r], xt, False, r == last, "E XT%d.%d" % (t, r), "@Z%d" % t)
+            mm(T["Z%d" % t][:, 0:256], T.E[:, 15 - r:143 - r], T["XT%d" % t][:, CH * r:CH * r + 256], False, r == last,
+               "E XT%d.%d" % (t, r), "@Z%d" % t)
 
-    def ak_out(t):
-        act(T.AKs[:], T["AK%d" % t][:, 0:8, :], "@AK%d" % t, "AKs")
+    def x_turn(t, rs, last=None, add_up=True):
+        for r in rs:
+            turn(T["XT%d" % t][:, CH * r:CH * r + 256], T["X%d" % t][:, 256 * r:256 * r + 256],
+                 "X%d.%d X%d.%d" % (t, 2 * r, t, 2 * r + 1), "XT%d.%d" % (t, r))
+            x_sum(t, [r] * add_up, last)
 
-    def offers(t, z, zname):
-        xt = " ".join("XT%d.%d" % (t, r) for r in range(16)) + " XT%dp XT%dq" % (t, t)
-        segmax(T.K1[:], z, zname, "K1")
-        copy(T.Ki[:], T.K1[:, 15::16], "K1", "Ki")
-        ts(T.Kf[:], T.Ki[:], 511, A_.bitwise_and, "Ki", "Kf")
-        ts(T.o1[:], T.Kf[:], -1.0, A_.mult, "Kf colr", "o1", colr, A_.add)
-        tt(T.K2a[:], T["XT%d" % t][:, 0:16 * CH].indirect(T.o1[:, 0:16]), T.AKs[:], A_.add, xt + " o1 AKs", "K2a")
-        turn(T.K2b[:], T.K2a[:], "K2a", "K2b")
-        segmax(T.K2[:], T.K2b[:], "K2b", "K2")
-        ts(T.KI[:], T.K2[:, 15::16], 65536.0, A_.mult, "K2", "KI", float(FLOOR), A_.max)
-        ts(T.M32[:, 0::3, :], T.KI[:], 4095, A_.bitwise_and, "KI", "Me")
-        ts(T.M32[:, 1:3, :], T.KI[:], 1, A_.arith_shift_right, "KI", "Mc", 2047, A_.bitwise_and)
+    def offers(t, z, zname, gap):
+        xt = " ".join("XT%d.%d" % (t, r) for r in range(16)) + " XT%d.p256 XT%d.p257" % (t, t)
+        for step in (
+            lambda: segmax(T.K1[:], z, zname, "K1"),
+            lambda: tt(T.Ki[:], T.K1[:, 15::16], T.Cs[:, 16 * t:16 * t + 16], A_.max, "K1 Cs0 Cs1", "Ki"),
+            lambda: ts(T.Kf[:], T.Ki[:], 511, A_.bitwise_and, "Ki", "Kf"),
+            lambda: ts(T.o1[:], T.Kf[:], -1.0, A_.mult, "Kf colr", "o1", colr, A_.add),
+            lambda: tt(T.K2a[:], T["XT%d" % t][:, 0:16 * CH].indirect(T.o1[:, 0:16]), T.AKs[:], A_.add,
+                       xt + " o1 AKs", "K2a"),
+            lambda: turn(T.K2b[:], T.K2a[:], "K2a", "K2b"),
+            lambda: segmax(T.K2[:], T.K2b[:], "K2b", "K2"),
+            lambda: ts(T.KI[:], T.K2[:, 15::16], 65536.0, A_.mult, "K2", "KI", float(FLOOR), A_.max),
+            lambda: (ts(T.M32[:, 0::3, :], T.KI[:], 4095, A_.bitwise_and, "KI", "Me"),
+                     ts(T.M32[:, 1:3, :], T.KI[:], 1, A_.arith_shift_right, "KI", "Mc", 2047, A_.bitwise_and)),
+        ):
+            step()
+            gap()
         copy(T["MU%d" % t][:], T.M32[:], "Me Mc", "MU%d" % t)
-        send(T["MU%d" % t], T["R%d" % t], 16, [rank + 1 + 2 * t, rank + 2 + 2 * t], "arr%d" % t, "MU%d" % t)
+        send(T["MU%d" % t], T["R%d" % t], 16, [rank + 1 + 2 * t, rank + 2 + 2 * t], "arr%d" % t, "MU%d" % t, STEP[t])
 
     def offered():
         ts(T.f4[:], T.KI[:], 12, A_.arith_shift_right, "KI", "f4", 15, A_.bitwise_and)
         copy(T.pio[:], T.f4[:], "f4", "pio")
 
     def place_row(t):
-        sc, bi = ((float(NONE), -24576.0), (0.5, -3.5))[t]
+        sc, bi = ((-float(NONE), 17.0 * NONE), (-1.0, 17.0))[t]
         act(T["OH%d" % t][:], T.DR[:, 0:16].indirect(T.pio[:, 0:16]), "DR pio", "OH%d" % t, sc, bi)
 
     def offer_row(t):
         act(T["OV%d" % t][:], T.OPP[:, 0:3088].indirect(T["MU%d" % t][:, 8:24]), "OPP0 OPP1 MU%d" % t, "OV%d" % t,
-            -1.0, 1537.0, SIGN)
+            1.0, -1537.0, SIGN)
 
     af_all = "Afd Af0 Af1 Af2"
     lf_all = "LFd LF0 LF1 LF2 LF3"
-    EBs = T.EB[:, 0:256]
+
+    def opposite(t, c0, c1, step=1, k=0):
+        bank, c = ("Z1", SP) if t and c0 >= SP else ("EB", 0)
+        rep = REP[t][c0 // SP]
+        return T[bank][:, rep * (c0 - c) + k:rep * (c1 - c):step], " @" + bank
+
+    def spread(t, b):
+        c0, c1, rep = SP * b, SP * b + SP, REP[t][b]
+        for k in range(rep):
+            mm(opposite(t, c0, c1, rep, k)[0], T.idf[:], T.Eb[:, c0:c1], True, True, "idf Eb%d" % b, opposite(t, c0, c1)[1])
 
     def candidates(t):
         R, rn = T["R%d" % t], "R%d" % t
-        mm(T.SC[:, 0:256], idb, T.NEG[:], True, False, "Sh NEG", "@SC")
-        mm(T.HR[:, 0:256], idb, T.DGc[:], True, False, "Sh DGc", "@HR")
-        mm(T.AK0[:, :, 0:16], idb, T.DGc[:], True, False, "Sh DGc", "@AK0")
-        mm(T.G[:, 0:272], idb, T.TH[:], True, False, "Sh TH THp", "@G")
         copy(T.cP[:], T.BK[:, 0:1544].indirect(R[:, 8:24]), "BK BKp " + rn, "cP")
         for b in range(2):
             act(T.Eb[:, 128 * b:128 * b + 128], T.OPP[:, 0:3088].indirect(R[:, 24 * b:24 * b + 8]), "OPP0 OPP1 " + rn,
-                "Eb%d" % b)
-        mm(EBs, T.idf[:], T.Eb[:], True, True, "idf Eb0 Eb1", "@EB")
-        for c0, c1 in ((0, OWN[t]), (OWN[t], 128), (128, 192), (192, 256)):
+                "Eb%d" % b, -1.0, float(NONE))
+            spread(t, b)
+        open_bank("SC", 0, EARLY[t] or 256)
+        cuts = (0, OWN[t]) + CUTS[t]
+        for c0, c1 in zip(cuts[:-1], cuts[1:]):
             (act if c0 else copy)(T.RAW[:, 16 * c0:16 * c1], T.Af[:, 256:2816].indirect(T.cP[:, c0:c1]),
-                                  "Af0 Af1 Af2 cP", "RAW.%d" % (c1 // 128 * c1))
-        ts(T.c16[:], T.cP[:], -1279.0, A_.add, "cP", "c16")
+                                  "Af0 Af1 Af2 cP", "RAW.%d" % c1)
+        ts(T.c16[:], T.cP[:], -2047.0, A_.add, "cP", "c16", UN, A_.mult)
 
-    def holders(c0, c1):
-        rd = "RAW.0 RAW.128" if c0 == 0 else "RAW.%d" % (c1 // 128 * c1)
-        for j in range(16):
-            eq = T.EQ[:, 256 * j + c0:256 * j + c1]
-            tt(eq, T.RAW[:, 16 * c0 + j:16 * c1:16], T.EB[:, c0:c1], A_.is_equal, rd + " @EB", "EQ.%d.%d" % (j, c0))
-            mm(T.SC[:, c0:c1], T.WJ[:, 128 * j:128 * j + 128], eq, False, c1 == 256 and j == 15,
-               "WJ.%d EQ.%d.%d" % (j, j, c0), "@SC")
+    def holders(t, k):
+        c0, c1 = ((0,) + CUTS[t])[k:k + 2]
+        b = c0 // SP
+        opp, bank = opposite(t, c0, c1)
+        rd = "RAW.%d RAW.%d" % (c0 or OWN[t], c1) + bank
+        rep, step = REP[t][b], 16 // REP[t][b]
+        m0 = max(c for c in (0,) + SUMS[t] if c <= c0)
+        for j in range(step):
+            at = 16 * SP * b + rep * (SP * j - SP * b) if t else rep * 256 * j
+            tt(T.EQ[:, at + rep * c0:at + rep * c1], T.RAW[:, 16 * c0 + j:16 * c1:step], opp, A_.is_equal,
+               rd, "EQ.%d.%d" % (j, k))
+            for h in range(rep * (c1 in SUMS[t])):
+                p = j + step * h
+                mm(T.SC[:, m0:c1], T.WJ[:, p::16], T.EQ[:, at + rep * m0 + h:at + rep * c1:rep], False,
+                   c1 in (EARLY[t], 256) and p == 15, "WJ.0 EQ.%d.%d" % (j, k), "@SC")
 
-    def first_holder():
-        tt(T.t32[:], T.SC[:, 0:256], T.c16[:], A_.min, "@SC c16", "t32")
-        ts(T.t16[:], T.t32[:], -1280.0, A_.max, "t32", "t16")
-        mm(T.HR[:, 0:256], T.BOh[:], T.t16[:], False, True, "BOh t16", "@HR")
-        mm(T.AK0[:, :, 0:16], T.BOh[:], T.t16[:], False, True, "BOh t16", "@AK0")
+    def open_bank(name, c0, c1):
+        if name == "SC":
+            mm(T.SC[:, c0:c1], idb, T.NV[:, 0:c1 - c0], True, False, "Sh NV", "@SC")
+        elif name == "G":
+            mm(T.G[:, 0:272], T.D16[0:16, 0:128], T.RT[0:16, :], True, False, "D16 RT", "@G")
+        else:
+            out, n = (T.Z0[:, c0:c1], c1 - c0) if name == "Z0" else (T.AK0[:, :, 0:16], 256)
+            mm(out, T.BO[:], T.OV[:, 0:n], True, False, "BO OV", "@" + name)
+            for _ in range(2):
+                mm(out, T.D16[0:16, 0:128], T.D16[0:16, 0:n], False, False, "D16", "@" + name)
 
-    def compare(t):
-        tt(T.h17[:, :, 1:17], T.HR[:, 0:256], T.DX[:], A_.subtract, "@HR DX", "h17")
-        segmax(T.hc[:], T.HR[:, 0:256], "@HR", "hc")
-        act(T.NF[:, :, 1:17], T.AK0[:, :, 0:16], "@AK0", "NF", -1.0, 1.0, RELU)
-        act(T.HD[:], T.AK0[:, :, 0:17], "@AK0", "HD")
-        for c in range(16):
-            n = 17 * (16 - c)
-            ts(T.EQ2[:, c, 0:n], T.h17[:, c:16, :], 5376.0, A_.add, "h17 h17p hc", "E2.%d" % c,
+    def first_holder(c0, c1):
+        b = c1 // 256
+        tt(T.t32[:, c0:c1], T.SC[:, c0:c1], T.c16[:, c0:c1], A_.min, "@SC c16", "t32.%d" % b)
+        yield
+        ts(T.t16[:, c0:c1], T.t32[:, c0:c1], -1.0, A_.max, "t32.%d" % b, "t16.%d" % b)
+        for out, name, start, stop in ((T.HR[:, c0:c1], "@HR", True, True), (T.Z0[:, c0:c1], "@Z0", False, True),
+                                       (T.AK0[:, c0 // 16:c1 // 16, 0:16], "@AK0", False, b == 1)):
+            mm(out, T.BO[:], T.t16[:, c0:c1], start, stop, "BO t16.%d" % b, name)
+        yield
+        ts(T.h17[:, c0 // 16:c1 // 16, 1:17], T.HR[:, c0:c1], 15.0, A_.add, "@HR", "h17.%d" % b)
+        scan(T.hc[:, c0:c1], T.RM[:, c0:c1], T.Z0[:, c0:c1], A_.mult, A_.max, "RM @Z0", "hc.%d" % b)
+        yield
+
+    def compare(k0, k1):
+        b = k1 // 16
+        for c in range(k1):
+            lo = max(c, k0)
+            out = T.EQ2[:, c, 17 * (lo - c):17 * (k1 - c)]
+            ts(out, T.h17[:, lo:k1, :], 3.0, A_.add, "h17.%d h17p hc.%d" % (b, b and c >= k0), "E2.%d.%d" % (c, b),
                T.hc[:, 16 * c + 15:16 * c + 16], A_.is_equal)
-            if c == 0:
-                ts(T.HO[:], T.hc[:, 15::16], -3841.0, A_.add, "hc", "HO")
+            if c == 0 and b == 1:
+                ts(T.HO[:], T.hc[:, 15::16], 1.0 / UN, A_.mult, "hc.0 hc.1", "HO", -3841.0, A_.add)
+                act(T.NF[:, :, 1:17], T.AK0[:, :, 0:16], "@AK0", "NF", -1.0 / UN, 1.0, RELU)
                 act(T.Acol[:], T.Af[:, 0:2816].indirect(T.HO[:, 0:16]), af_all + " HO", "Acol")
-            if c < 15:
-                mm(T.G[:, 17 + 17 * c:272], T.LO[:], T.EQ2[:, c, 17:n], False, False, "LO E2.%d" % c, "@G")
-            if c == 11:
-                mm(T.G[:, 0:272], T.LO[:], T.NF[:], False, False, "LO NF NFp", "@G")
-        mm(T.G[:, 0:272], T.LT[:], T.EQ2[:, :, 0:17], False, True, "LT " + " ".join("E2.%d" % c for c in range(16)), "@G")
-        tt(T.eqb[:], T.Acol[:], EBs, (A_.is_equal, A_.not_equal)[t], "Acol @EB", "eqb")
+                act(T.HD[:], T.AK0[:, :, 0:17], "@AK0", "HD", -0.25)
+            lo = max(c + 1, k0)
+            if lo < k1:
+                mm(T.G[:, 17 * lo:17 * k1], T.BO[:], T.EQ2[:, c, 17 * (lo - c):17 * (k1 - c)], False, False,
+                   "BO E2.%d.%d" % (c, b), "@G")
+            if c == 9 and b == 1:
+                mm(T.G[:, 0:272], T.BO[:], T.NF[:], False, False, "BO NF NFp", "@G")
+        mm(T.G[:, 17 * k0:17 * k1], T.LT[:], T.EQ2[:, k0:k1, 0:17], False, b == 1,
+           "LT " + " ".join("E2.%d.%d" % (c, b) for c in range(k0, k1)), "@G")
+
+    def differs(t):
+        for c0, c1 in ((0, SP), (SP, 256)) if t else ((0, 256),):
+            opp, bank = opposite(t, c0, c1, REP[t][c0 // SP])
+            tt((T.nef, T.neb)[t][:, c0:c1], T.Acol[:, c0:c1], opp, A_.not_equal, "Acol" + bank, "ne")
 
     def columns():
-        scan(T.Fk[:], T.G[:, 0:272], T.HD[:], A_.min, A_.max, "@G HD", "Fk")
-        ts(T.SO[:], T.Fk[:, 16::17], -3841.0, A_.add, "Fk", "SO")
+        scan(T.Fk[:], T.G[:, 0:272], T.HD[:], A_.max, A_.min, "@G HD", "Fk")
+        ts(T.SO[:], T.Fk[:, 16::17], -4.0 / UN, A_.mult, "Fk", "SO", -3841.0, A_.add)
 
     def verdicts(t):
         ac = T["ac%d" % t]
@@ -349,121 +390,152 @@ def rank_program(g, core, T, topo):
     def said(t, q):
         sd, ps = T["sd%d" % t], T.SC[:, 0:256]
         mm(ps, idb, T["OV%d" % t][:], True, False, "Sh OV%d" % t, "@SC")
-        mm(ps, T.BOq[:], T["AC%d" % t][:, :, 1:17], False, True, "BOq AC%d" % t, "@SC")
-        act(sd[:], ps, "@SC", "sd%d" % t, 2.0, -8.0, RELU)
+        mm(ps, idb, T["OV%d" % t][:], False, False, "Sh OV%d" % t, "@SC")
+        mm(ps, T.BO[:], T["AC%d" % t][:, :, 1:17], False, True, "BO AC%d" % t, "@SC")
+        act(sd[:], ps, "@SC", "sd%d" % t, -0.5, -7.0)
         dma(q, T.said[:, 256 * t:256 * t + 256], sd[0::16, :], "sd%d" % t, "out%d" % t, "o%d" % t)
 
     def left(lo, hi, rd, wr):
-        act(T.LF[:, lo:hi], T.Af[:, lo:hi], rd, wr, -1.0, float(NONE), SIGN)
+        act(T.LF[:, lo:hi], T.Af[:, lo:hi], rd, wr, 1.0, 0.0, SIGN)
 
-    act(T.idf[:], idb, "Sh", "idf")
-    capital(0)
-    act(T.B15[:], idb, "Sh b15", "B15", b15)
-    act(T.W0f[:], T.Sh[:], "Sh n0", "W0f", n0)
-    act(T.W1f[:], T.Sh[:], "Sh n1", "W1f", n1)
     ak_open(0)
     z_open(0)
-    act(T.DG[:], T.D16[:, 0:16].indirect(T.rl[:, 0:16]), "D16 rl", "DG")
-    capital(1)
-    ak_out(0)
-    act(T.AK0[:, :, 16], T.K16[:], "K16 colD", "@AK0", 1.0, colD)
-    act(T.Af[:, 256:512], T.Ap0[:], "Ap0", "Af0")
-    act(T.Af[:, 512:768], T.Ap1[:], "Ap1", "Af1")
-    act(T.DGc[:], T.DG[:], "DG", "DGc", 4096.0, 20480.0)
-    act(T.TH[:, :, 1:17], T.DG[:], "DG", "TH", 8192.0 - BIG, float(BIG))
     x_gather("V", 0, 0, 2)
     x_gather("S", 0, 6, 8)
     x_turn(0, (0, 1))
     x_gather("V", 0, 2, 4)
     x_gather("S", 0, 8, 10)
     x_turn(0, (2, 3, 6, 7))
-    x_gather("V", 0, 4, 6)
-    for r0, r1 in ((10, 12), (12, 14), (14, 15), (15, 16)):
+    x_gather("V", 0, 4, 5.5)
+    for r0, r1 in ((10, 12), (12, 14), (5.5, 6), (14, 15), (15, 16)):
         x_gather("S", 0, r0, r1)
-    x_turn(0, (4, 5, 8, 9, 10, 11, 12, 13, 14, 15), 15)
-    for r0, r1 in ((0, 4), (4, 8), (8, 10)):
+    x_turn(0, (4, 8, 9, 10, 11, 12, 13, 5, 14, 15), 15)
+    act(T.AKs[:], T.AK0[:, 0:8, :], "@AK0", "AKs")
+    act(T.AK0[:, :, 16], T.PLf[:], "PLf", "@AK0", UN, 3841.0 * UN)
+    sel(T.D16[0:16, :], T.OV[0:16, :], [[0, 16], [1, 16]], A_.is_equal, 0, -1, "OV", "D16")
+    x_gather("S", 1, 0, 3)
+    done = [512]
+
+    def widen(n=GAP):
+        c = done[0]
+        if n:
+            ts(T.Af[:, 256 + c:256 + c + n], T.A[:, c:c + n], -1.0, A_.mult, "A2.%d" % (c >= 1536),
+               "Af2.%d" % c + " Af2" * (c + n == 2560), float(NONE), A_.add)
+        done[0] += n
+    for u in range(2):
+        ts(T.Cs[:, u::2], T.capT[:, 16 * u:16 * u + 16], 512.0, A_.mult, "capT", "Cs%d" % u, 512.0, A_.add)
+    ts(colr, T.PLa[:, 0:1], CH / 16.0, A_.mult, "PLa", "colr", 256.0, A_.add)
+    offers(0, T.Z0[:, 0:256], "@Z0", widen)
+    for r0, r1 in ((3, 6), (6, 9), (9, 11), (11, 12)):
         x_gather("S", 1, r0, r1)
-    offers(0, T.Z0[:, 0:256], "@Z0")
+    act(T.idf[:], idb, "Sh", "idf")
     ak_open(1)
     z_open(1)
-    sel(T.LT[:], T.BO[:], [[1, 128]], A_.is_gt, 0, -1, "BO", "LT0")
+    for name in ("Z0", "AK0"):
+        open_bank(name, 0, EARLY[0] or 256)
+
+    iota(T.BK[:, 1536:1544], [[0, 8]], 0, 0, "", "BKp", False)
+    fill(T.NV[:], 256, -1, "NV")
+    fill(T.RT[0:16, 0:272], 272, -512, "RT")
+    sel(T.RT[0:16, 0:272], T.RT[0:16, 0:272], [[0, 16], [1, 17]], A_.not_equal, -1, -1, "RT", "RT", -0.875)
+    iota(T.RT[0:16, 0:272:17], [[0, 16]], 512, 0, "RT", "RT")
+    iota(T.K16[:], [[-16, 16]], 240, 0, "", "K16")
+    sel(T.LT[:], T.BO[:], [[1, 128]], A_.is_gt, 0, -1, "BO", "LT")
     fill(T.NF[:, :, 0], 16, 0, "NFp")
     fill(T.Af[:, 0:256], 256, 0, "Afd")
     fill(T.Y[:, 512:768], 256, 0, "Y")
-    fill(T.LF[:, 0:256], 256, 0, "LFd")
-
-    copy(T.Af[:, 768:2816], T.A[:, 512:2560], "A2", "Af2")
+    for x in (256, 257):
+        fill(T.XT1[:, x::CH], 16, 0, "XT1.p%d" % x)
+    fill(T.C128[:], 160, 128, "C128")
+    sel(T.C128[:], T.C128[:], [[-1, 160]], A_.is_equal, 16, 1, "C128", "C128")
+    sel(T.W0b[:], T.C128[:], [[0, 5], [1, 2], [0, 16]], A_.is_equal, -1, 0, "C128", "W0b")
+    sel(T.W1b[:], T.C128[:], [[0, 5], [1, 2], [0, 16]], A_.is_equal, 0, 0, "C128", "W1b")
+    widen(1536 - done[0])
+    widen(1024)
     offered()
-    x_turn(1, range(0, 6))
+    memset(T.h17[:, :, 0], 2.0, "h17p")
+    x_turn(1, range(0, TURN))
 
-    candidates(0)
-    x_turn(1, range(6, 10))
-    holders(0, 128)
-    copy(T.r32[:], T.R0[:], "R0", "r32")
-    ts(T.q1[:], T.r32[:, 1:3, :], 4.0, A_.mult, "r32", "q1", 1.0, A_.add)
-    holders(128, 192)
-    tt(T.q2[:], T.q1[:], T.r32[:, 0::3, :], A_.subtract, "q1 r32", "q2")
-    copy(T.oo[:], T.q2[:], "q2", "oo")
-    holders(192, 256)
-    act(T.DX[:], T.DG[:], "DG", "DX", 4096.0, 1280.0)
-    act(T.LO[:], T.BO[:], "BO", "LO", -2.0 ** 14)
-    for r0 in (10, 12, 14):
-        x_gather("S", 1, r0, r0 + 2)
-    act(T.LT[:], T.LT[:], "LT0", "LT", -2.0 ** 14)
-    first_holder()
-    x_turn(1, (10, 11))
-    compare(0)
-    act(T.BO5[:], T.BO[:], "BO", "BO5", 512.0)
-    act(T.eqf[:], T.eqb[:], "eqb", "eqf", float(NONE))
-    mm(T.Z0[:, 0:256], T.BO5[:], T.eqb[:], True, True, "BO5 eqb", "@Z0")
-    act(T.Lo[:], T.L[:, 0:3088].indirect(T.oo[:, 0:16]), "L Lp oo", "Lo")
-    act(T.cn[:], T.Z0[:, 0:256], "@Z0", "cn")
-    act(T.W0b[:], T.Sh[:], "Sh k0", "W0b", k0)
-    act(T.W1b[:], T.Sh[:], "Sh k1", "W1b", k1)
+    def judge(t, gaps):
+        n, sp = 2, EARLY[t]
+        for name in ("AK0", "G", "Z0") * t:
+            open_bank(name, 0, sp or 256)
+        candidates(t)
+        for k in range(n):
+            gaps[k]()
+            holders(t, k)
+            if k == t == 0:
+                open_bank("G", 0, 256)
+        gaps[n]()
+        if sp:
+            early = first_holder(0, sp)
+            next(early)
+            next(early)
+            open_bank("SC", sp, 256)
+        holders(t, n)
+        if sp:
+            next(early)
+            open_bank("Z0", sp, 256)
+            compare(0, sp // 16)
+        for k in range(n + 1, len(CUTS[t])):
+            holders(t, k)
+        gaps[n + 1]()
+        for k, _ in enumerate(first_holder(sp, 256)):
+            gaps[n + 2 + k]()
+        compare(sp // 16, 16)
+        differs(t)
+
+    def nothing():
+        pass
+    judge(0, [lambda: (x_turn(1, range(TURN, 12), None, False), copy(T.r32[:], T.R0[:], "R0", "r32")),
+              lambda: ts(T.q1[:], T.r32[:, 1:3, :], 4.0, A_.mult, "r32", "q1", 1.0, A_.add),
+              lambda: tt(T.q2[:], T.q1[:], T.r32[:, 0::3, :], A_.subtract, "q1 r32", "q2"),
+              lambda: (x_gather("S", 1, 12, 14), x_gather("S", 1, 14, 16), act(T.BOf[:], T.BO[:], "BO", "BOf")),
+              lambda: (copy(T.oo[:], T.q2[:], "q2", "oo"),
+                       act(T.Lo[:], T.L[:, 0:3088].indirect(T.oo[:, 0:16]), "L Lp oo", "Lo")),
+              lambda: x_turn(1, (12, 13), None, False),
+              lambda: ts(T.DR[:], T.K16[:], T.PLf[:, 0:1], A_.is_equal, "K16 PLf", "DR")])
+    mm(T.Z0[:, 0:256], T.BOf[:], T.nef[:], True, True, "BOf ne", "@Z0")
+    x_sum(1, range(TURN, 14))
+    act(T.BOa[:], T.BO[:], "BO", "BOa", float(NONE))
+    act(T.cn[:], T.Z0[:, 0:256], "@Z0", "cn", -512.0, 8192.0)
     columns()
-    tt(T.Af[:, 0:2816].indirect(T.SO[:, 0:16]), T.Acol[:], T.eqf[:], A_.max, "SO Acol eqf", af_all)
-    x_turn(1, (12, 13, 14, 15), 15)
+    tt(T.Af[:, 0:2816].indirect(T.SO[:, 0:16]), T.Acol[:], T.nef[:], A_.mult, "SO Acol ne", af_all)
+    x_turn(1, (14, 15), 15)
     tt(T.Y[:, 0:2816].indirect(T.SO[:, 0:16]), T.Lo[:], T.cn[:], A_.mult, "SO Lo cn", "Y")
     verdicts(0)
-    act(T.Pen[:], T.Af[:, 512:768], "Af1", "Pen", 512.0, -512.0 * (NONE - 1), RELU)
-    swap(1, T.W0b, T.W1b, T.Pen, "W0b W1b Pen", True)
+    fill(T.LF[:, 0:256], 256, 0, "LFd")
     place_row(0)
-    ak_out(1)
+    act(T.Pen[:], T.Af[:, 512:768], "Af1", "Pen", 1.0, -0.5, SIGN)
+    swap(1, T.W0b, T.W1b, lambda be: T.Pen[:, :, be, :], "W0b W1b Pen", True)
+    offer_row(0)
+    act(T.AKs[:], T.AK1[:, 0:8, :], "@AK1", "AKs", 1.0, -128.0)
 
     turn(T.YT[:], T.Y[:, 512:768], "Y", "YT")
     tt(T.Zc[:], T.Z1[:, 0:256], T.YT[:], A_.subtract, "@Z1 YT", "Zc")
-    act(T.BOa[:], T.BO[:], "BO", "BOa", 1536.0)
-    act(T.BOq[:], T.BO[:], "BO", "BOq", 0.25)
-    offer_row(0)
     mm(T.Z0[:, 0:256], idb, T.OH0[:], True, False, "Sh OH0", "@Z0")
     mm(T.Z0[:, 0:256], T.BOa[:], T.AC0[:, :, 1:17], False, True, "BOa AC0", "@Z0")
-    left(512, 1792, "Af1 Af2", "LF1 LF2")
+    left(512, 2304, "Af1 Af2", "LF1 LF2")
     said(0, "Y")
-    offers(1, T.Zc[:], "Zc")
-    tt(T.Af[:, 256:512], T.Af[:, 256:512], T.Z0[:, 0:256], A_.max, "Af0 @Z0", "Af0")
+    offers(1, T.Zc[:], "Zc", nothing)
+    tt(T.Af[:, 256:512], T.Af[:, 256:512], T.Z0[:, 0:256], A_.min, "Af0 @Z0", "Af0")
     offered()
 
-    candidates(1)
-    for c0, c1 in ((0, 128), (128, 192), (192, 256)):
-        holders(c0, c1)
-    left(256, 512, "Af0", "LF0")
-    left(1792, 2816, "Af2", "LF3")
-    place_row(1)
-    first_holder()
-    compare(1)
-    act(T.lc[:], T.Acol[:], "Acol", "lc", -1.0, float(NONE), SIGN)
+    judge(1, [nothing] * 3
+          + [lambda: (left(256, 512, "Af0", "LF0"), left(2304, 2816, "Af2", "LF3"), place_row(1))] + [nothing] * 3)
+    act(T.lc[:], T.Acol[:], "Acol", "lc", 1.0, 0.0, SIGN)
     offer_row(1)
     mm(T.Z0[:, 0:256], idb, T.OH1[:], True, False, "Sh OH1", "@Z0")
     columns()
     verdicts(1)
-    tt(T.LF[:, 0:2816].indirect(T.SO[:, 0:16]), T.lc[:], T.eqb[:], A_.mult, "SO lc eqb", lf_all)
+    tt(T.LF[:, 0:2816].indirect(T.SO[:, 0:16]), T.lc[:], T.neb[:], A_.mult, "SO lc ne", lf_all)
     dma("Y", T.left[:, 512:2560], T.LF[:, 768:2816], "LF2 LF3", "out2", "o2")
     dma("S", T.left[:, 0:256], T.LF[:, 256:512], "LF0", "out3", "o3")
-    mm(T.Z0[:, 0:256], T.BOq[:], T.AC1[:, :, 1:17], False, True, "BOq AC1", "@Z0")
-    tt(T.LG[:], T.LF[:, 512:768], T.Z0[:, 0:256], A_.is_gt, "LF1 @Z0", "LG")
+    mm(T.Z0[:, 0:256], T.BO[:], T.AC1[:, :, 1:17], False, True, "BO AC1", "@Z0")
+    tt(T.LG[:], T.LF[:, 512:768], T.Z0[:, 0:256], A_.min, "LF1 @Z0", "LG")
     dma("Y", T.left[:, 256:512], T.LG[:], "LG", "out4", "o4")
     said(1, "S")
     add("Y", None, "out0 out1 out2 out3 out4", "")
 
-    _emit(ops, {"V": V, "S": S, "P": P, "G": g, "Y": g.sync}, T)
-    g.wait_ge(T.sem.sent, 64)
+    _emit(ops, {"V": V, "S": S, "P": P, "G": g, "Y": g.sync}, T, engines)
+    g.wait_ge(T.sem.sent, sum(engines.values()))

from concourse.bass import DstId, RemoteDMATransfer
from concourse.mybir import AluOpType, ActivationFunctionType

F, B, I, U, H = "float32", "bfloat16", "int32", "uint16", "float16"
N = 8
CH = 258
NONE = 3072
FLOOR = 15 * 4096 + NONE
UN = 2.0 ** -11
OWN = (24, 40)
CUTS = ((96, 160, 216, 256), (80, 128, 176, 224, 256))
SUMS = CUTS
SP = 128
EARLY = (0, 128)
GAP = 0
REP = ((2, 2), (2, 2))
STEP = (1, 1)
TURN = 6

_SB = {
    B: "L:3088 Sh:160 C128:160 W0b:160 W1b:160 B15:128 BO:128 BOa:128 LT:128 E:144 DR:16 D16:256 RT:272 "
       "NV:256 PAY:256 RM:256 OV:256 Ut:256 WJ:2048 X0:4096 X1:4096 XT0:4128 XT1:4128 "
       "OH0:256 OH1:256 OV0:256 OV1:256 EQ:4096 NF:16,17 EQ2:16,272 ac0:16,17 ac1:16,17 AC0:16,17 AC1:16,17 neb:256 "
       "Pen:8,2,16 LF:2816 lc:256 LG:256",
    F: "capF:32 capT:32 Cs:32 col:4 PLf:16 idf:128 W0f:160 W1f:160 K16:16 OPP:3088 Af:2816 Ap:16,2,16 "
       "AKs:256 K1:256 K2a:256 K2b:256 K2:256 Eb:256 RAW:4096 t32:256 hc:256 HD:272 Fk:272 Acol:256 nef:256 BOf:128 cn:256 "
       "r32:4,8 q1:16 q2:16 Lo:256 Y:2816 YT:256 Zc:256 sd0:256 sd1:256",
    I: "A:2560 BK:1544 capI:32 PL:16 PLa:16 Ki:16 Kf:16 KI:16 M32:4,8 f4:16",
    U: "PLu:16 Off:512 o1:16 MU0:32 MU1:32 R0:32 R1:32 pio:16 cP:256 HO:16 SO:16 oo:16",
    H: "h17:16,17 c16:256 t16:256",
}
SCRATCH = {e.split(":")[0]: ("sbuf", [128] + [int(x) for x in e.split(":")[1].split(",")], dt)
           for dt, names in _SB.items() for e in names.split()}
SCRATCH.update({k: ("psum", [128, 512], F) for k in ("Z0", "Z1", "SC", "HR", "G", "EB")})
SCRATCH.update({k: ("psum", [128, 16, 32], F) for k in ("AK0", "AK1")})
DMAS = ["dA0", "dL", "dcap", "dA2", "dA3", "dBK", "dAf", "dWJ", "o0", "o1", "o2", "o3", "o4"]
SEMAPHORES = ["cV", "cS", "cP", "cG", "sent", "arr0", "arr1", "ack0", "ack1"] + DMAS


def _emit(ops, queues, T, arrivals):
    writer, readers, bank = {}, {}, {}
    known = {q: set() for q in queues}
    snap, waits, needed = [], [], set()
    earlier = {q: [] for q in queues}
    for n, (q, fn, rd, wr, sem) in enumerate(ops):
        deps = set()
        for k in rd + wr:
            if k in writer:
                deps.add(writer[k])
            if k[0] == "@":
                deps.update(m for e, m in bank.get(k, {}).items() if e != q)
        for k in wr:
            deps.update(readers.get(k, []))
        mine = []
        for m in sorted(deps, reverse=True):
            if m in known[q] or (q == "P" and ops[m][0] == "P"):
                continue
            mine.append(m)
            needed.add(m)
            known[q] |= snap[m]
        waits.append(mine)
        for k in rd:
            readers.setdefault(k, []).append(n)
        for k in wr:
            writer[k] = n
            readers[k] = []
        for k in rd + wr:
            if k[0] == "@":
                bank.setdefault(k, {})[q] = n
        if sem is None:
            earlier[q].append(n)
            snap.append(known[q] | set(earlier[q]))
        else:
            snap.append(known[q] | {m for m, o in enumerate(ops) if o[4] == sem})
    count, at = {q: 0 for q in queues}, {}
    for n, (q, fn, rd, wr, sem) in enumerate(ops):
        if sem is not None:
            at[n] = (sem, arrivals.get(sem, 16) * sum(1 for o in ops if o[4] == sem))
        elif n in needed:
            count[q] += 1
            at[n] = ("c" + q, count[q])
    for n, (q, fn, rd, wr, sem) in enumerate(ops):
        for m in waits[n]:
            queues[q].wait_ge(T.sem[at[m][0]], at[m][1])
        if fn is None:
            continue
        ins = fn()
        if ins is None:
            continue
        if sem is not None:
            ins.then_inc(T.sem[sem], 16)
        elif n in needed:
            ins.then_inc(T.sem["c" + q], 1)


def rank_program(g, core, T, topo):
    rank = T.rank_of(core)
    if rank is None:
        return
    A_ = AluOpType
    ID, RELU, SIGN = ActivationFunctionType.Identity, ActivationFunctionType.Relu, ActivationFunctionType.Sign
    V, S, P = g.vector, g.scalar, g.tensor
    ops, engines = [], {}

    def add(q, fn, rd, wr, sem=None):
        ops.append((q, fn, rd.split(), wr.split(), sem))

    def memset(ap, c, wr):
        add("V", lambda: V.memset(ap, c), "", wr)

    def copy(o, i, rd, wr):
        add("V", lambda: V.tensor_copy(o, i), rd, wr)

    def ts(o, i, s1, o0, rd, wr, s2=None, o1=None):
        if o1 is None:
            add("V", lambda: V.tensor_scalar(o, i, s1, None, o0), rd, wr)
        else:
            add("V", lambda: V.tensor_scalar(o, i, s1, s2, o0, o1), rd, wr)

    def tt(o, a, b, op, rd, wr):
        add("V", lambda: V.tensor_tensor(o, a, b, op), rd, wr)

    def scan(o, d0, d1, o0, o1, rd, wr):
        add("V", lambda: V.tensor_tensor_scan(o, d0, d1, 0.0, o0, o1), rd, wr)

    def segmax(o, i, rd, wr):
        scan(o, T.RM[:], i, A_.mult, A_.max, rd + " RM", wr)

    def turn(o, i, rd, wr):
        add("V", lambda: V.transpose(o, i), rd, wr)

    def act(o, i, rd, wr, scale=1.0, bias=0.0, func=ID):
        add("S", lambda: S.activation(o, i, func, bias=bias, scale=scale), rd, wr)

    def mm(o, l, r, start, stop, rd, wr):
        add("P", lambda: P.matmul(o, l, r, start, stop), rd, wr)

    def iota(o, pat, base, cm, rd, wr, small=True):
        if small:
            add("G", lambda: g.iota(o, pat, base, cm, allow_small_or_imprecise_dtypes=True), rd, wr)
        else:
            add("G", lambda: g.iota(o, pat, base, cm), rd, wr)

    def fill(o, n, c, wr):
        iota(o, [[0, n]], c, 0, "", wr)

    def sel(o, i, pat, cmp, base, cm, rd, wr, other=0.0):
        add("G", lambda: g.affine_select(o, i, pat, cmp, other, base, cm), rd, wr)

    def dma(q, o, i, rd, wr, sem):
        add(q, lambda: (g.sync if q == "Y" else g.scalar).dma_start(o, i), rd, wr, sem)

    def send(src, dst, width, peers, sem, rd, step=1):
        trs = []
        for b, peer in enumerate(peers):
            c = T.cores[peer % N]
            eng = topo.engines(core, c)
            half = eng[b * len(eng) // 2:(b + 1) * len(eng) // 2:step]
            engines[sem] = engines.get(sem, 0) + len(half)
            rid, pid = topo.addr(c)[:2]
            trs.append(RemoteDMATransfer(dst_ids=[DstId(rid=rid, pnc=pid)], dma_engine_mask=sum(1 << e for e in half),
                                         remote_sem=T.sem[sem], src=src[:, b * width:(b + 1) * width],
                                         dst=dst[:, b * width:(b + 1) * width]))

        def go():
            g.remote_dma_fused(trs, local_sem=T.sem.sent)
        add("G", go, rd, "")

    for t in range(2):
        add("G", None, "", "R%d" % t, "arr%d" % t)
        add("G", None, "", "AC%d" % t, "ack%d" % t)

    dma("Y", T.A[:, 0:512], T.acct[:, 0:512], "", "A01 go", "dA0")
    dma("S", T.capI[:], T.cap[:, :], "", "capI", "dcap")
    dma("Y", T.L[:, 0:3072], T.loss[:, :], "", "L", "dL")
    dma("Y", T.A[:, 512:1536], T.acct[:, 512:1536], "go", "A2.0", "dA2")
    dma("Y", T.A[:, 1536:2560], T.acct[:, 1536:2560], "", "A2.1", "dA3")
    dma("Y", T.BK[:, 0:1536], T.book[:, :], "", "BK", "dBK")

    idb = T.Sh[:, 16:144]
    colr, b15, n0, n1 = [T.col[:, k:k + 1] for k in range(4)]
    memset(T.OV[:], 1.0, "OV")
    memset(T.Ut[:], 0.0, "Ut")
    iota(T.PL[:], [[1, 16]], 0, 16, "", "PL", False)
    iota(T.OPP[:, 0:96], [[2, 48], [-1, 2]], 1, 0, "", "OPP0")
    sel(T.Sh[:], T.OV[:, 0:160], [[-1, 160]], A_.is_equal, 16, 1, "OV", "Sh")
    sel(T.BO[:], T.OV[:, 0:128], [[-16, 8], [0, 16]], A_.is_ge, 0, 1, "OV", "BO")
    sel(T.BO[:], T.BO[:], [[16, 8], [0, 16]], A_.is_ge, 15, -1, "BO", "BO")
    iota(T.PAY[:], [[-1, 256]], 256, 0, "", "PAY")
    iota(T.Ut[0:16, :], [[-64, 16], [64, 16]], 2, 0, "", "Ut")
    sel(T.Ut[0:16, :], T.Ut[0:16, :], [[1, 16], [-1, 16]], A_.is_ge, 0, 0, "Ut", "Ut")
    for x in (256, 257):
        fill(T.XT0[:, x::CH], 16, 0, "XT0.p%d" % x)
    iota(T.OPP[:, 1536:3088], [[2, 776], [-1, 2]], 1537, 0, "", "OPP1")

    memset(T.RM[:], 1.0, "RM")
    ts(T.PLa[:], T.PL[:], 255, A_.bitwise_and, "PL", "PLa")
    ts(T.f4[:, 0:1], T.PL[:, 0:1], 8, A_.arith_shift_right, "PL", "f4", 1, A_.bitwise_and)
    memset(T.RM[:, 0::16], 0.0, "RM")
    copy(T.PLu[:], T.PLa[:], "PLa", "PLu")
    ts(n1, T.f4[:, 0:1], -2.0 ** -16, A_.mult, "f4", "n1")
    ts(n0, T.f4[:, 0:1], 2.0 ** -16, A_.mult, "f4", "n0", -2.0 ** -16, A_.add)
    ts(b15, T.PLa[:, 0:1], -1.0 / 256, A_.mult, "PLa", "b15", 15.0 / 16 + NONE / 65536, A_.add)
    copy(T.capF[:], T.capI[:], "capI", "capF")
    memset(T.L[:, 3072:3088], 0.0, "Lp")
    turn(T.capT[:], T.capF[:], "capF", "capT")
    memset(T.E[:], 0.0, "E")
    copy(T.PLf[:], T.PLa[:], "PLa", "PLf")
    copy(T.Off[:, 0:256], T.A[:, 0:256].indirect(T.PLu[:, 0:16]), "A01 PLu", "Off0")
    ts(T.Ap[:], T.A[:, 0:512], -1.0, A_.mult, "A01", "Ap", float(NONE), A_.add)
    copy(T.Off[:, 256:512], T.A[:, 256:512].indirect(T.PLu[:, 0:16]), "A01 PLu", "Off1")
    ts(T.E[:, 15:143:16], T.BO[:, 0::16], 512.0, A_.mult, "BO", "E")
    for k in (96, 192):
        act(T.OPP[:, k:2 * k], T.OPP[:, 0:k], "OPP0", "OPP0", 1.0, float(k))
    act(T.B15[:], idb, "Sh b15", "B15", b15)
    act(T.W0f[:], T.Sh[:], "Sh n0", "W0f", n0)
    act(T.W1f[:], T.Sh[:], "Sh n1", "W1f", n1)
    for k in (384, 768):
        act(T.OPP[:, k:2 * k], T.OPP[:, 0:k], "OPP0", "OPP0", 1.0, float(k))
    dma("Y", T.Af[:, 256:768], T.Ap[:], "Ap", "Af0 Af1", "dAf")
    for k in range(8):
        dma("Y", T.WJ[16 * k:128, 256 * k:256 * k + 256], T.Ut[0:128 - 16 * k, :], "Ut", "WJ.%d" % k, "dWJ")
        if k:
            dma("Y", T.WJ[0:16 * k, 256 * k:256 * k + 256], T.Ut[16:16 + 16 * k, :], "Ut", "WJ0.%d" % k, "dWJ")

    def swap(t, w0, w1, src, names, stop):
        ak = T["AK%d" % t]
        for u, be, l in ((0, 0, w0[:, 16:144]), (0, 1, w0[:, 0:128]), (1, 1, w1[:, 16:144]), (1, 0, w1[:, 32:160])):
            mm(ak[:, 0:8, 16 * u:16 * u + 16], l, src(be), False, stop and u == 1 and be == 0, names, "@AK%d" % t)

    def ak_open(t):
        mm(T["AK%d" % t][:, 0:8, :], T.B15[:], T.OV[:], True, False, "B15 OV", "@AK%d" % t)
        swap(t, T.W0f, T.W1f, lambda be: T.Ap[:, 8 * t:8 * t + 8, be, :], "W0f W1f Ap", t == 0)

    def z_open(t):
        mm(T["Z%d" % t][:, 0:256], idb, T.PAY[:], True, False, "Sh PAY", "@Z%d" % t)

    def x_gather(q, t, r0, r1):
        h0, h1 = int(2 * r0), int(2 * r1)
        src = T.L[:, 0:3088].indirect(T.Off[:, 256 * t + 8 * h0:256 * t + 8 * h1])
        dst = T["X%d" % t][:, 128 * h0:128 * h1]
        if h1 > h0:
            (copy if q == "V" else act)(dst, src, "L Lp Off%d" % t, " ".join("X%d.%d" % (t, h) for h in range(h0, h1)))

    def x_sum(t, rs, last=None):
        for r in rs:
            mm(T["Z%d" % t][:, 0:256], T.E[:, 15 - r:143 - r], T["XT%d" % t][:, CH * r:CH * r + 256], False, r == last,
               "E XT%d.%d" % (t, r), "@Z%d" % t)

    def x_turn(t, rs, last=None, add_up=True):
        for r in rs:
            turn(T["XT%d" % t][:, CH * r:CH * r + 256], T["X%d" % t][:, 256 * r:256 * r + 256],
                 "X%d.%d X%d.%d" % (t, 2 * r, t, 2 * r + 1), "XT%d.%d" % (t, r))
            x_sum(t, [r] * add_up, last)

    def offers(t, z, zname, gap):
        xt = " ".join("XT%d.%d" % (t, r) for r in range(16)) + " XT%d.p256 XT%d.p257" % (t, t)
        for step in (
            lambda: segmax(T.K1[:], z, zname, "K1"),
            lambda: tt(T.Ki[:], T.K1[:, 15::16], T.Cs[:, 16 * t:16 * t + 16], A_.max, "K1 Cs0 Cs1", "Ki"),
            lambda: ts(T.Kf[:], T.Ki[:], 511, A_.bitwise_and, "Ki", "Kf"),
            lambda: ts(T.o1[:], T.Kf[:], -1.0, A_.mult, "Kf colr", "o1", colr, A_.add),
            lambda: tt(T.K2a[:], T["XT%d" % t][:, 0:16 * CH].indirect(T.o1[:, 0:16]), T.AKs[:], A_.add,
                       xt + " o1 AKs", "K2a"),
            lambda: turn(T.K2b[:], T.K2a[:], "K2a", "K2b"),
            lambda: segmax(T.K2[:], T.K2b[:], "K2b", "K2"),
            lambda: ts(T.KI[:], T.K2[:, 15::16], 65536.0, A_.mult, "K2", "KI", float(FLOOR), A_.max),
            lambda: (ts(T.M32[:, 0::3, :], T.KI[:], 4095, A_.bitwise_and, "KI", "Me"),
                     ts(T.M32[:, 1:3, :], T.KI[:], 1, A_.arith_shift_right, "KI", "Mc", 2047, A_.bitwise_and)),
        ):
            step()
            gap()
        copy(T["MU%d" % t][:], T.M32[:], "Me Mc", "MU%d" % t)
        send(T["MU%d" % t], T["R%d" % t], 16, [rank + 1 + 2 * t, rank + 2 + 2 * t], "arr%d" % t, "MU%d" % t, STEP[t])

    def offered():
        ts(T.f4[:], T.KI[:], 12, A_.arith_shift_right, "KI", "f4", 15, A_.bitwise_and)
        copy(T.pio[:], T.f4[:], "f4", "pio")

    def place_row(t):
        sc, bi = ((-float(NONE), 17.0 * NONE), (-1.0, 17.0))[t]
        act(T["OH%d" % t][:], T.DR[:, 0:16].indirect(T.pio[:, 0:16]), "DR pio", "OH%d" % t, sc, bi)

    def offer_row(t):
        act(T["OV%d" % t][:], T.OPP[:, 0:3088].indirect(T["MU%d" % t][:, 8:24]), "OPP0 OPP1 MU%d" % t, "OV%d" % t,
            1.0, -1537.0, SIGN)

    af_all = "Afd Af0 Af1 Af2"
    lf_all = "LFd LF0 LF1 LF2 LF3"

    def opposite(t, c0, c1, step=1, k=0):
        bank, c = ("Z1", SP) if t and c0 >= SP else ("EB", 0)
        rep = REP[t][c0 // SP]
        return T[bank][:, rep * (c0 - c) + k:rep * (c1 - c):step], " @" + bank

    def spread(t, b):
        c0, c1, rep = SP * b, SP * b + SP, REP[t][b]
        for k in range(rep):
            mm(opposite(t, c0, c1, rep, k)[0], T.idf[:], T.Eb[:, c0:c1], True, True, "idf Eb%d" % b, opposite(t, c0, c1)[1])

    def candidates(t):
        R, rn = T["R%d" % t], "R%d" % t
        copy(T.cP[:], T.BK[:, 0:1544].indirect(R[:, 8:24]), "BK BKp " + rn, "cP")
        for b in range(2):
            act(T.Eb[:, 128 * b:128 * b + 128], T.OPP[:, 0:3088].indirect(R[:, 24 * b:24 * b + 8]), "OPP0 OPP1 " + rn,
                "Eb%d" % b, -1.0, float(NONE))
            spread(t, b)
        open_bank("SC", 0, EARLY[t] or 256)
        cuts = (0, OWN[t]) + CUTS[t]
        for c0, c1 in zip(cuts[:-1], cuts[1:]):
            (act if c0 else copy)(T.RAW[:, 16 * c0:16 * c1], T.Af[:, 256:2816].indirect(T.cP[:, c0:c1]),
                                  "Af0 Af1 Af2 cP", "RAW.%d" % c1)
        ts(T.c16[:], T.cP[:], -2047.0, A_.add, "cP", "c16", UN, A_.mult)

    def holders(t, k):
        c0, c1 = ((0,) + CUTS[t])[k:k + 2]
        b = c0 // SP
        opp, bank = opposite(t, c0, c1)
        rd = "RAW.%d RAW.%d" % (c0 or OWN[t], c1) + bank
        rep, step = REP[t][b], 16 // REP[t][b]
        m0 = max(c for c in (0,) + SUMS[t] if c <= c0)
        for j in range(step):
            at = 16 * SP * b + rep * (SP * j - SP * b) if t else rep * 256 * j
            tt(T.EQ[:, at + rep * c0:at + rep * c1], T.RAW[:, 16 * c0 + j:16 * c1:step], opp, A_.is_equal,
               rd, "EQ.%d.%d" % (j, k))
            for h in range(rep * (c1 in SUMS[t])):
                p = j + step * h
                mm(T.SC[:, m0:c1], T.WJ[:, p::16], T.EQ[:, at + rep * m0 + h:at + rep * c1:rep], False,
                   c1 in (EARLY[t], 256) and p == 15, "WJ.0 EQ.%d.%d" % (j, k), "@SC")

    def open_bank(name, c0, c1):
        if name == "SC":
            mm(T.SC[:, c0:c1], idb, T.NV[:, 0:c1 - c0], True, False, "Sh NV", "@SC")
        elif name == "G":
            mm(T.G[:, 0:272], T.D16[0:16, 0:128], T.RT[0:16, :], True, False, "D16 RT", "@G")
        else:
            out, n = (T.Z0[:, c0:c1], c1 - c0) if name == "Z0" else (T.AK0[:, :, 0:16], 256)
            mm(out, T.BO[:], T.OV[:, 0:n], True, False, "BO OV", "@" + name)
            for _ in range(2):
                mm(out, T.D16[0:16, 0:128], T.D16[0:16, 0:n], False, False, "D16", "@" + name)

    def first_holder(c0, c1):
        b = c1 // 256
        tt(T.t32[:, c0:c1], T.SC[:, c0:c1], T.c16[:, c0:c1], A_.min, "@SC c16", "t32.%d" % b)
        yield
        ts(T.t16[:, c0:c1], T.t32[:, c0:c1], -1.0, A_.max, "t32.%d" % b, "t16.%d" % b)
        for out, name, start, stop in ((T.HR[:, c0:c1], "@HR", True, True), (T.Z0[:, c0:c1], "@Z0", False, True),
                                       (T.AK0[:, c0 // 16:c1 // 16, 0:16], "@AK0", False, b == 1)):
            mm(out, T.BO[:], T.t16[:, c0:c1], start, stop, "BO t16.%d" % b, name)
        yield
        ts(T.h17[:, c0 // 16:c1 // 16, 1:17], T.HR[:, c0:c1], 15.0, A_.add, "@HR", "h17.%d" % b)
        scan(T.hc[:, c0:c1], T.RM[:, c0:c1], T.Z0[:, c0:c1], A_.mult, A_.max, "RM @Z0", "hc.%d" % b)
        yield

    def compare(k0, k1):
        b = k1 // 16
        for c in range(k1):
            lo = max(c, k0)
            out = T.EQ2[:, c, 17 * (lo - c):17 * (k1 - c)]
            ts(out, T.h17[:, lo:k1, :], 3.0, A_.add, "h17.%d h17p hc.%d" % (b, b and c >= k0), "E2.%d.%d" % (c, b),
               T.hc[:, 16 * c + 15:16 * c + 16], A_.is_equal)
            if c == 0 and b == 1:
                ts(T.HO[:], T.hc[:, 15::16], 1.0 / UN, A_.mult, "hc.0 hc.1", "HO", -3841.0, A_.add)
                act(T.NF[:, :, 1:17], T.AK0[:, :, 0:16], "@AK0", "NF", -1.0 / UN, 1.0, RELU)
                act(T.Acol[:], T.Af[:, 0:2816].indirect(T.HO[:, 0:16]), af_all + " HO", "Acol")
                act(T.HD[:], T.AK0[:, :, 0:17], "@AK0", "HD", -0.25)
            lo = max(c + 1, k0)
            if lo < k1:
                mm(T.G[:, 17 * lo:17 * k1], T.BO[:], T.EQ2[:, c, 17 * (lo - c):17 * (k1 - c)], False, False,
                   "BO E2.%d.%d" % (c, b), "@G")
            if c == 9 and b == 1:
                mm(T.G[:, 0:272], T.BO[:], T.NF[:], False, False, "BO NF NFp", "@G")
        mm(T.G[:, 17 * k0:17 * k1], T.LT[:], T.EQ2[:, k0:k1, 0:17], False, b == 1,
           "LT " + " ".join("E2.%d.%d" % (c, b) for c in range(k0, k1)), "@G")

    def differs(t):
        for c0, c1 in ((0, SP), (SP, 256)) if t else ((0, 256),):
            opp, bank = opposite(t, c0, c1, REP[t][c0 // SP])
            tt((T.nef, T.neb)[t][:, c0:c1], T.Acol[:, c0:c1], opp, A_.not_equal, "Acol" + bank, "ne")

    def columns():
        scan(T.Fk[:], T.G[:, 0:272], T.HD[:], A_.max, A_.min, "@G HD", "Fk")
        ts(T.SO[:], T.Fk[:, 16::17], -4.0 / UN, A_.mult, "Fk", "SO", -3841.0, A_.add)

    def verdicts(t):
        ac = T["ac%d" % t]
        act(ac[:], T.G[:, 0:272], "@G", "ac%d" % t, 1.0, 0.0, SIGN)
        send(ac, T["AC%d" % t], 8, [rank - 1 - 2 * t, rank - 2 - 2 * t], "ack%d" % t, "ac%d" % t)

    def said(t, q):
        sd, ps = T["sd%d" % t], T.SC[:, 0:256]
        mm(ps, idb, T["OV%d" % t][:], True, False, "Sh OV%d" % t, "@SC")
        mm(ps, idb, T["OV%d" % t][:], False, False, "Sh OV%d" % t, "@SC")
        mm(ps, T.BO[:], T["AC%d" % t][:, :, 1:17], False, True, "BO AC%d" % t, "@SC")
        act(sd[:], ps, "@SC", "sd%d" % t, -0.5, -7.0)
        dma(q, T.said[:, 256 * t:256 * t + 256], sd[0::16, :], "sd%d" % t, "out%d" % t, "o%d" % t)

    def left(lo, hi, rd, wr):
        act(T.LF[:, lo:hi], T.Af[:, lo:hi], rd, wr, 1.0, 0.0, SIGN)

    ak_open(0)
    z_open(0)
    x_gather("V", 0, 0, 2)
    x_gather("S", 0, 6, 8)
    x_turn(0, (0, 1))
    x_gather("V", 0, 2, 4)
    x_gather("S", 0, 8, 10)
    x_turn(0, (2, 3, 6, 7))
    x_gather("V", 0, 4, 5.5)
    for r0, r1 in ((10, 12), (12, 14), (5.5, 6), (14, 15), (15, 16)):
        x_gather("S", 0, r0, r1)
    x_turn(0, (4, 8, 9, 10, 11, 12, 13, 5, 14, 15), 15)
    act(T.AKs[:], T.AK0[:, 0:8, :], "@AK0", "AKs")
    act(T.AK0[:, :, 16], T.PLf[:], "PLf", "@AK0", UN, 3841.0 * UN)
    sel(T.D16[0:16, :], T.OV[0:16, :], [[0, 16], [1, 16]], A_.is_equal, 0, -1, "OV", "D16")
    x_gather("S", 1, 0, 3)
    done = [512]

    def widen(n=GAP):
        c = done[0]
        if n:
            ts(T.Af[:, 256 + c:256 + c + n], T.A[:, c:c + n], -1.0, A_.mult, "A2.%d" % (c >= 1536),
               "Af2.%d" % c + " Af2" * (c + n == 2560), float(NONE), A_.add)
        done[0] += n
    for u in range(2):
        ts(T.Cs[:, u::2], T.capT[:, 16 * u:16 * u + 16], 512.0, A_.mult, "capT", "Cs%d" % u, 512.0, A_.add)
    ts(colr, T.PLa[:, 0:1], CH / 16.0, A_.mult, "PLa", "colr", 256.0, A_.add)
    offers(0, T.Z0[:, 0:256], "@Z0", widen)
    for r0, r1 in ((3, 6), (6, 9), (9, 11), (11, 12)):
        x_gather("S", 1, r0, r1)
    act(T.idf[:], idb, "Sh", "idf")
    ak_open(1)
    z_open(1)
    for name in ("Z0", "AK0"):
        open_bank(name, 0, EARLY[0] or 256)

    iota(T.BK[:, 1536:1544], [[0, 8]], 0, 0, "", "BKp", False)
    fill(T.NV[:], 256, -1, "NV")
    fill(T.RT[0:16, 0:272], 272, -512, "RT")
    sel(T.RT[0:16, 0:272], T.RT[0:16, 0:272], [[0, 16], [1, 17]], A_.not_equal, -1, -1, "RT", "RT", -0.875)
    iota(T.RT[0:16, 0:272:17], [[0, 16]], 512, 0, "RT", "RT")
    iota(T.K16[:], [[-16, 16]], 240, 0, "", "K16")
    sel(T.LT[:], T.BO[:], [[1, 128]], A_.is_gt, 0, -1, "BO", "LT")
    fill(T.NF[:, :, 0], 16, 0, "NFp")
    fill(T.Af[:, 0:256], 256, 0, "Afd")
    fill(T.Y[:, 512:768], 256, 0, "Y")
    for x in (256, 257):
        fill(T.XT1[:, x::CH], 16, 0, "XT1.p%d" % x)
    fill(T.C128[:], 160, 128, "C128")
    sel(T.C128[:], T.C128[:], [[-1, 160]], A_.is_equal, 16, 1, "C128", "C128")
    sel(T.W0b[:], T.C128[:], [[0, 5], [1, 2], [0, 16]], A_.is_equal, -1, 0, "C128", "W0b")
    sel(T.W1b[:], T.C128[:], [[0, 5], [1, 2], [0, 16]], A_.is_equal, 0, 0, "C128", "W1b")
    widen(1536 - done[0])
    widen(1024)
    offered()
    memset(T.h17[:, :, 0], 2.0, "h17p")
    x_turn(1, range(0, TURN))

    def judge(t, gaps):
        n, sp = 2, EARLY[t]
        for name in ("AK0", "G", "Z0") * t:
            open_bank(name, 0, sp or 256)
        candidates(t)
        for k in range(n):
            gaps[k]()
            holders(t, k)
            if k == t == 0:
                open_bank("G", 0, 256)
        gaps[n]()
        if sp:
            early = first_holder(0, sp)
            next(early)
            next(early)
            open_bank("SC", sp, 256)
        holders(t, n)
        if sp:
            next(early)
            open_bank("Z0", sp, 256)
            compare(0, sp // 16)
        for k in range(n + 1, len(CUTS[t])):
            holders(t, k)
        gaps[n + 1]()
        for k, _ in enumerate(first_holder(sp, 256)):
            gaps[n + 2 + k]()
        compare(sp // 16, 16)
        differs(t)

    def nothing():
        pass
    judge(0, [lambda: (x_turn(1, range(TURN, 12), None, False), copy(T.r32[:], T.R0[:], "R0", "r32")),
              lambda: ts(T.q1[:], T.r32[:, 1:3, :], 4.0, A_.mult, "r32", "q1", 1.0, A_.add),
              lambda: tt(T.q2[:], T.q1[:], T.r32[:, 0::3, :], A_.subtract, "q1 r32", "q2"),
              lambda: (x_gather("S", 1, 12, 14), x_gather("S", 1, 14, 16), act(T.BOf[:], T.BO[:], "BO", "BOf")),
              lambda: (copy(T.oo[:], T.q2[:], "q2", "oo"),
                       act(T.Lo[:], T.L[:, 0:3088].indirect(T.oo[:, 0:16]), "L Lp oo", "Lo")),
              lambda: x_turn(1, (12, 13), None, False),
              lambda: ts(T.DR[:], T.K16[:], T.PLf[:, 0:1], A_.is_equal, "K16 PLf", "DR")])
    mm(T.Z0[:, 0:256], T.BOf[:], T.nef[:], True, True, "BOf ne", "@Z0")
    x_sum(1, range(TURN, 14))
    act(T.BOa[:], T.BO[:], "BO", "BOa", float(NONE))
    act(T.cn[:], T.Z0[:, 0:256], "@Z0", "cn", -512.0, 8192.0)
    columns()
    tt(T.Af[:, 0:2816].indirect(T.SO[:, 0:16]), T.Acol[:], T.nef[:], A_.mult, "SO Acol ne", af_all)
    x_turn(1, (14, 15), 15)
    tt(T.Y[:, 0:2816].indirect(T.SO[:, 0:16]), T.Lo[:], T.cn[:], A_.mult, "SO Lo cn", "Y")
    verdicts(0)
    fill(T.LF[:, 0:256], 256, 0, "LFd")
    place_row(0)
    act(T.Pen[:], T.Af[:, 512:768], "Af1", "Pen", 1.0, -0.5, SIGN)
    swap(1, T.W0b, T.W1b, lambda be: T.Pen[:, :, be, :], "W0b W1b Pen", True)
    offer_row(0)
    act(T.AKs[:], T.AK1[:, 0:8, :], "@AK1", "AKs", 1.0, -128.0)

    turn(T.YT[:], T.Y[:, 512:768], "Y", "YT")
    tt(T.Zc[:], T.Z1[:, 0:256], T.YT[:], A_.subtract, "@Z1 YT", "Zc")
    mm(T.Z0[:, 0:256], idb, T.OH0[:], True, False, "Sh OH0", "@Z0")
    mm(T.Z0[:, 0:256], T.BOa[:], T.AC0[:, :, 1:17], False, True, "BOa AC0", "@Z0")
    left(512, 2304, "Af1 Af2", "LF1 LF2")
    said(0, "Y")
    offers(1, T.Zc[:], "Zc", nothing)
    tt(T.Af[:, 256:512], T.Af[:, 256:512], T.Z0[:, 0:256], A_.min, "Af0 @Z0", "Af0")
    offered()

    judge(1, [nothing] * 3
          + [lambda: (left(256, 512, "Af0", "LF0"), left(2304, 2816, "Af2", "LF3"), place_row(1))] + [nothing] * 3)
    act(T.lc[:], T.Acol[:], "Acol", "lc", 1.0, 0.0, SIGN)
    offer_row(1)
    mm(T.Z0[:, 0:256], idb, T.OH1[:], True, False, "Sh OH1", "@Z0")
    columns()
    verdicts(1)
    tt(T.LF[:, 0:2816].indirect(T.SO[:, 0:16]), T.lc[:], T.neb[:], A_.mult, "SO lc ne", lf_all)
    dma("Y", T.left[:, 512:2560], T.LF[:, 768:2816], "LF2 LF3", "out2", "o2")
    dma("S", T.left[:, 0:256], T.LF[:, 256:512], "LF0", "out3", "o3")
    mm(T.Z0[:, 0:256], T.BO[:], T.AC1[:, :, 1:17], False, True, "BO AC1", "@Z0")
    tt(T.LG[:], T.LF[:, 512:768], T.Z0[:, 0:256], A_.min, "LF1 @Z0", "LG")
    dma("Y", T.left[:, 256:512], T.LG[:], "LG", "out4", "o4")
    said(1, "S")
    add("Y", None, "out0 out1 out2 out3 out4", "")

    _emit(ops, {"V": V, "S": S, "P": P, "G": g, "Y": g.sync}, T, engines)
    g.wait_ge(T.sem.sent, sum(engines.values()))
